import numpy as np
import ml_dtypes


def mxq(x, axis, fmt="e4m3"):
    dtype, down = {"e4m3": (ml_dtypes.float8_e4m3fn, 7), "e5m2": (ml_dtypes.float8_e5m2, 14)}[fmt]
    v = np.moveaxis(np.asarray(x, np.float32).astype(ml_dtypes.bfloat16).astype(np.float64), axis, -1)
    blocks = v.reshape(v.shape[:-1] + (-1, 32))
    amax = np.abs(blocks).max(-1, keepdims=True)
    byte = np.maximum(np.where(amax > 0, np.frexp(amax)[1] - 1 + 127, 0) - down, 1)
    scale = np.exp2(byte - 127.0)
    codes = (blocks / scale).astype(np.float32).astype(dtype).astype(np.float64)
    return np.moveaxis((codes * scale).reshape(v.shape), -1, axis)


WIDE = False


def mx_kscale(k):
    if not WIDE:
        return np.ones(k)
    levels = np.array([10, -10, 5, -5, 0])
    if k % 512:
        return np.exp2(np.random.permutation(np.resize(levels, k // 32))).repeat(32)
    a = np.empty((k // 512, 16))
    for p in range(k // 512):
        a[p, :8] = np.random.permutation(np.resize(levels, 8))
        for g in range(8):
            far = levels[np.abs(levels - a[p, g]) >= 10]
            a[p, g + 8] = far[np.random.randint(len(far))]
    return np.exp2(a.ravel()).repeat(32)


BF16 = ml_dtypes.bfloat16


def bf(x):
    return np.asarray(x, np.float32).astype(BF16)


def f64(x):
    return np.asarray(x).astype(np.float64)


E2M1 = np.array([0.0, 0.5, 1.0, 1.5, 2.0, 3.0, 4.0, 6.0, -0.0, -0.5, -1.0, -1.5, -2.0, -3.0, -4.0, -6.0])


def pack_weight(w, fmt):
    k, n = w.shape
    w = f64(bf(w)).reshape(k // 32, 32, n)
    amax = np.abs(w).max(1)
    if fmt == "e4m3":
        byte = np.frexp(amax)[1] - 1 + 127 - 7
    else:
        mant, ex = np.frexp(amax / 6.0)
        byte = np.where(mant > 0.5, ex, ex - 1) + 127
    byte = np.clip(np.where(amax > 0, byte, 1), 1, 254)
    scaled = (w * np.exp2(127.0 - byte)[:, None, :]).reshape(k, n).astype(np.float32)
    by_word = np.ascontiguousarray(scaled.reshape(k // 512, 128, 4, n).transpose(0, 1, 3, 2))
    if fmt == "e4m3":
        words = by_word.astype(ml_dtypes.float8_e4m3fn).view(np.uint8)
    else:
        c = by_word.astype(ml_dtypes.float4_e2m1fn).view(np.uint8) & 0xF
        words = c[..., 0::2] | (c[..., 1::2] << 4)
    return np.ascontiguousarray(words), np.ascontiguousarray(byte.astype(np.uint8).reshape(k // 512, 16, n))


def unpack_weight(words, scales, fmt):
    g, p, n, _ = words.shape
    if fmt == "e4m3":
        vals = np.ascontiguousarray(words).view(ml_dtypes.float8_e4m3fn).astype(np.float64)
    else:
        nib = np.empty((g, p, n, 4), np.uint8)
        nib[..., 0::2] = words & 0xF
        nib[..., 1::2] = words >> 4
        vals = E2M1[nib]
    vals = vals * np.repeat(np.exp2(scales.astype(np.float64) - 127.0), 8, axis=1)[..., None]
    return vals.transpose(0, 1, 3, 2).reshape(g * 512, n)
def pack4(w):
    words, scales = pack_weight(w, "e2m1")
    return words.reshape(words.shape[0], 128, -1), scales


def unpack4(words, scales):
    return unpack_weight(words.reshape(words.shape[0], 128, -1, 2), scales, "e2m1")


def planes(Y):
    n, m = Y.shape
    b = f64(bf(Y)).reshape(n // 32, 32, m)
    amax = np.abs(b).max(1)
    byte = np.clip(np.where(amax > 0, np.frexp(amax)[1] - 1 + 127 - 7, 1), 1, 254)
    codes = (b * np.exp2(127.0 - byte)[:, None, :]).reshape(n, m).astype(np.float32).astype(ml_dtypes.float8_e4m3fn).view(np.uint8)
    words = codes.reshape(n // 512, 128, 4, m).transpose(0, 1, 3, 2)
    return np.ascontiguousarray(words), np.ascontiguousarray(byte.astype(np.uint8).reshape(n // 512, 16, m))


M, C, F, N = 1024, 4096, 512, 2048

def setup_inputs():
    s = mx_kscale(C)
    t = mx_kscale(F)
    sst = np.random.randn(M, C) * s[None, :]
    size = np.exp(0.5 * np.random.randn(F))
    E = np.random.randn(C, F) / np.sqrt(C) * size[None, :]
    patterns_words, patterns_scales = pack4(E / s[:, None])
    centre = 0.3 * np.random.randn(F) * size
    inv_scale = t / size
    R = np.random.randn(F, N) / np.sqrt(F)
    regression_words, regression_scales = pack4(R / t[:, None])
    bias = 0.3 * np.random.randn(N)
    rain_spread = np.exp(0.8 * np.random.randn(N))
    return {"sst": bf(sst), "patterns_words": patterns_words, "patterns_scales": patterns_scales,
            "centre": bf(centre), "inv_scale": bf(inv_scale),
            "regression_words": regression_words, "regression_scales": regression_scales,
            "bias": bf(bias), "rain_spread": bf(rain_spread)}

def reference(sst, patterns_words, patterns_scales, centre, inv_scale, regression_words, regression_scales, bias, rain_spread):
    E = unpack4(patterns_words, patterns_scales)
    R = unpack4(regression_words, regression_scales)
    A = mxq(f64(sst), 1, "e4m3") @ E
    Z = (A - f64(centre)) * f64(inv_scale)
    y = ((mxq(Z, 1, "e4m3") @ R) + f64(bias)) * f64(rain_spread)
    Y = y.T
    words, scales = planes(Y)
    return y, words, scales

@@ -1,0 +1,407 @@
+from contextlib import ExitStack
+
+import concourse.mybir as mybir
+from concourse.masks import make_identity
+
+M, C, F, N = 1024, 4096, 512, 2048
+FLOPS = 2 * M * C * F + 2 * M * F * N
+
+F32 = mybir.dt.float32
+BF16 = mybir.dt.bfloat16
+I32 = mybir.dt.int32
+U32 = mybir.dt.uint32
+U8 = mybir.dt.uint8
+FP8X4 = mybir.dt.float8_e4m3fn_x4
+FP4X4 = mybir.dt.float4_e2m1fn_x4
+ALU = mybir.AluOpType
+ACT = mybir.ActivationFunctionType
+
+P = 128
+HALVES = 16
+UNITS = 16
+CH = 256
+SPLIT = "-------" + "v" * 9
+X_BUFS = 16
+RING = 7
+
+
+def tile_sst_pattern_rainfall_projection_h1_kernel(
+    tc, sst, patterns_words, patterns_scales, centre, inv_scale,
+    regression_words, regression_scales, bias, rain_spread, out_0, out_1, out_2,
+):
+    nc = tc.nc
+    with ExitStack() as ctx:
+        keep = ctx.enter_context(tc.tile_pool(name="keep", bufs=1))
+        work = ctx.enter_context(tc.tile_pool(name="work", bufs=1))
+        psum = ctx.enter_context(tc.psum_pool(name="psum", bufs=1))
+        ctx.enter_context(tc.manual_schedule())
+
+        counts = {}
+
+        def rot(pool, tag, depth, shape, dtype):
+            k = counts.get(tag, 0)
+            counts[tag] = k + 1
+            slot = "%s%d" % (tag, k % depth)
+            if pool is psum:
+                return pool.tile(shape, dtype, name=slot, tag=slot)
+            return pool.tile(shape, dtype, name=slot, tag=slot, align_bytes=64)
+
+        ident = keep.tile([P, P], F32, align_bytes=64)
+        e_words = [keep.tile([P, 4, 2 * F], U8, name="e_words%d" % j, align_bytes=64) for j in range(2)]
+        e_scales = keep.tile([P, 8, F], U8, align_bytes=64)
+        r_raw = keep.tile([P, 2 * N], U8, align_bytes=64)
+        rs_raw = keep.tile([P, N], U8, align_bytes=64)
+        r_words = [keep.tile([P, 4, 2 * P], U8, name="r_words%d" % g, align_bytes=64) for g in range(4)]
+        r_scales = keep.tile([P, 16, P], U8, align_bytes=64)
+        centre_raw = keep.tile([P, 4], BF16, align_bytes=64)
+        inv_raw = keep.tile([P, 4], BF16, align_bytes=64)
+        bias_raw = keep.tile([P, 4, 4], BF16, align_bytes=64)
+        spread_raw = keep.tile([P, 4, 4], BF16, align_bytes=64)
+        centre_col = keep.tile([P, 4], F32, align_bytes=64)
+        inv_col = keep.tile([P, 4], F32, align_bytes=64)
+        spread_col = keep.tile([P, 16], F32, align_bytes=64)
+        shift_col = keep.tile([P, 16], F32, align_bytes=64)
+        centre_row = keep.tile([P, F], F32, align_bytes=64)
+        inv_row = keep.tile([P, F], F32, align_bytes=64)
+        y_scales = [
+            keep.tile([P, 4, 3 * CH], U8, name="y_scales0", align_bytes=64),
+            keep.tile([P, 4, CH], U8, name="y_scales1", align_bytes=64),
+        ]
+
+        nc.vector.memset(e_scales[:].rearrange("p g n -> p (g n)").bitcast(I32), 0)
+        nc.scalar.dma_start(out=centre_raw[:], in_=centre.rearrange("(p t) -> p t", t=4))
+        nc.scalar.dma_start(out=inv_raw[:], in_=inv_scale.rearrange("(p t) -> p t", t=4))
+        make_identity(nc, ident[:])
+        nc.vector.memset(rs_raw[:].bitcast(I32), 0)
+        for q in range(4):
+            nc.gpsimd.dma_start(
+                out=rs_raw[32 * q : 32 * q + 4, :].bitcast(I32),
+                in_=regression_scales[0, 4 * q : 4 * q + 4, :].bitcast(I32),
+            )
+        nc.gpsimd.dma_start(out=spread_raw[:], in_=rain_spread.rearrange("(g p t) -> p g t", p=P, t=4))
+        nc.gpsimd.dma_start(out=bias_raw[:], in_=bias.rearrange("(g p t) -> p g t", p=P, t=4))
+
+        x_raw = {}
+
+        def load_x(h):
+            i, j = divmod(h, 2)
+            x_raw[h] = rot(work, "x_raw", X_BUFS, [P, 2048], BF16)
+            nc.sync.dma_start(out=x_raw[h][:], in_=sst[P * i : P * (i + 1), 2048 * j : 2048 * (j + 1)])
+
+        def load_e(j):
+            nc.sync.dma_start(
+                out=e_words[j][:].bitcast(I32),
+                in_=patterns_words[4 * j : 4 * j + 4].rearrange("g p n -> p g n").bitcast(I32),
+            )
+
+        load_x(0)
+        for q in range(4):
+            nc.sync.dma_start(
+                out=e_scales[32 * q : 32 * q + 4].bitcast(I32),
+                in_=patterns_scales[:, 4 * q : 4 * q + 4, :].rearrange("g r n -> r g n").bitcast(I32),
+            )
+        load_e(0)
+        load_x(1)
+        load_e(1)
+        load_x(2)
+        load_x(3)
+        nc.sync.dma_start(out=r_raw[:].bitcast(I32), in_=regression_words[0].bitcast(I32))
+        for h in range(4, HALVES):
+            load_x(h)
+
+        nc.scalar.activation(out=centre_col[:], in_=centre_raw[:], func=ACT.Identity)
+        nc.vector.tensor_copy(out=inv_col[:], in_=inv_raw[:])
+
+        x_split, x_t, x_q = {}, {}, {}
+        acc, z_diff, z_bf, z_t, z_q = {}, {}, {}, {}, {}
+        y_t, y_bf, y_out = {}, {}, {}
+
+        def move(on_vector, dst, src):
+            if on_vector:
+                nc.vector.tensor_copy(out=dst, in_=src)
+            else:
+                nc.scalar.copy(out=dst, in_=src)
+
+        def split_words(h):
+            if SPLIT[h] == "-":
+                return
+            x_split[h] = rot(work, "x_split", 2, [P, 2, 512], F32)
+            move(
+                SPLIT[h] == "v",
+                x_split[h][:].rearrange("m u (c i) -> m c u i", i=4),
+                x_raw[h][:].bitcast(F32).rearrange("m (c i u) -> m c u i", i=4, u=2),
+            )
+
+        def transpose_x(h):
+            x_t[h] = rot(work, "x_t", 3, [P, 4, P, 2], F32)
+            banks = []
+            for b in range(2):
+                bank = rot(psum, "ring", RING, [P, 2, 2, P], F32)
+                banks.append(bank)
+                for gg in range(2):
+                    g = 2 * b + gg
+                    for u in range(2):
+                        if SPLIT[h] != "-":
+                            src = x_split[h][:, u, P * g : P * (g + 1)]
+                        else:
+                            src = x_raw[h][:].bitcast(F32)[:, 256 * g + u : 256 * (g + 1) : 2]
+                        nc.tensor.transpose(bank[:, gg, u, :], src, ident[:])
+            return banks
+
+        def copy_x(h, banks, b, on_vector):
+            move(on_vector, x_t[h][:, 2 * b : 2 * b + 2], banks[b][:].rearrange("p g u m -> p g m u"))
+
+        def quantise_x(h):
+            codes = rot(work, "x_codes", 3, [P, 4 * P], U32)
+            scales = rot(work, "x_scales", 3, [P, 4 * P], U8)
+            x_q[h] = (codes, scales)
+            nc.vector.quantize_mx(
+                out=codes[:].bitcast(FP8X4),
+                scales=scales[:],
+                in_=x_t[h][:].rearrange("p g m u -> p (g m u)").bitcast(BF16),
+            )
+
+        def stage1(h):
+            i, j = divmod(h, 2)
+            if j == 0:
+                acc[i] = rot(psum, "acc", 1, [P, F], F32)
+            codes, scales = x_q[h]
+            for gg in range(4):
+                g = 4 * j + gg
+                nc.tensor.matmul_mx(
+                    out=acc[i][:],
+                    lhsT=codes[:, P * gg : P * (gg + 1)].bitcast(FP8X4),
+                    lhsT_scale=scales[:, P * gg : P * (gg + 1)],
+                    rhs=e_words[j][:, gg, :].bitcast(FP4X4),
+                    rhs_scale=e_scales[:, g, :],
+                    start=(g == 0),
+                    stop=(g == 7),
+                )
+
+        def centre_z(i):
+            z_diff[i] = rot(work, "z_diff", 1, [P, F], F32)
+            nc.vector.tensor_tensor(
+                out=z_diff[i][:].rearrange("m (u p e) -> m u p e", u=2, e=2),
+                in0=acc[i][:].rearrange("m (p u e) -> m u p e", u=2, e=2),
+                in1=centre_row[:].rearrange("m (u p e) -> m u p e", u=2, e=2),
+                op=ALU.subtract,
+            )
+
+        def scale_z(i):
+            z_bf[i] = rot(work, "z_bf", 2, [P, F], BF16)
+            nc.vector.tensor_tensor(out=z_bf[i][:], in0=z_diff[i][:], in1=inv_row[:], op=ALU.mult)
+
+        def transpose_z(i):
+            bank = rot(psum, "ring", RING, [P, 2, P], F32)
+            for u in range(2):
+                nc.tensor.transpose(bank[:, u, :], z_bf[i][:].bitcast(F32)[:, P * u : P * (u + 1)], ident[:])
+            z_t[i] = rot(work, "z_t", 2, [P, P, 2], F32)
+            nc.scalar.copy(out=z_t[i][:], in_=bank[:].rearrange("p u m -> p m u"))
+
+        def quantise_z(i):
+            c, s = divmod(i, 2)
+            if s == 0:
+                z_q[c] = (rot(work, "z_codes", 2, [P, CH], U32), rot(work, "z_scales", 2, [P, CH], U8))
+            codes, scales = z_q[c]
+            nc.vector.quantize_mx(
+                out=codes[:, P * s : P * (s + 1)].bitcast(FP8X4),
+                scales=scales[:, P * s : P * (s + 1)],
+                in_=z_t[i][:].rearrange("p m u -> p (m u)").bitcast(BF16),
+            )
+
+        def stage2(un):
+            c, g = divmod(un, 4)
+            codes, scales = z_q[c]
+            banks = []
+            for b in range(2):
+                bank = rot(psum, "ring", RING, [P, 2, CH], F32)
+                banks.append(bank)
+                for tt in range(2):
+                    t = 2 * b + tt
+                    nc.tensor.matmul_mx(
+                        out=bank[:, tt, :],
+                        lhsT=r_words[g][:, t, :].bitcast(FP4X4),
+                        lhsT_scale=r_scales[:, 4 * g + t, :],
+                        rhs=codes[:].bitcast(FP8X4),
+                        rhs_scale=scales[:],
+                        start=True,
+                        stop=True,
+                    )
+            y_t[un] = rot(work, "y_t", 3, [P, 4, CH], F32)
+            return banks
+
+        def affine(un, banks, b, on_vector):
+            g = un % 4
+            for tt in range(2):
+                t = 2 * b + tt
+                col = slice(4 * g + t, 4 * g + t + 1)
+                if on_vector:
+                    nc.vector.tensor_scalar(
+                        out=y_t[un][:, t, :], in0=banks[b][:, tt, :], scalar1=spread_col[:, col],
+                        scalar2=shift_col[:, col], op0=ALU.mult, op1=ALU.add,
+                    )
+                else:
+                    nc.scalar.activation(
+                        out=y_t[un][:, t, :], in_=banks[b][:, tt, :], func=ACT.Identity,
+                        bias=shift_col[:, col], scale=spread_col[:, col],
+                    )
+
+        def interleave_y(un):
+            y_bf[un] = rot(work, "y_bf", 2, [P, CH, 4], BF16)
+            nc.vector.tensor_copy(
+                out=y_bf[un][:].rearrange("p (c i) t -> p c t i", i=4),
+                in_=y_t[un][:].rearrange("p t (c i) -> p c t i", i=4),
+            )
+
+        def quantise_y(un):
+            c, g = divmod(un, 4)
+            codes = rot(work, "y_codes", 4, [P, CH], U32)
+            if c < 3:
+                scales = y_scales[0][:, g, CH * c : CH * (c + 1)]
+            else:
+                scales = y_scales[1][:, g, :]
+            nc.vector.quantize_mx(
+                out=codes[:].bitcast(FP8X4), scales=scales, in_=y_bf[un][:].rearrange("p m t -> p (m t)")
+            )
+            nc.sync.dma_start(
+                out=out_1[g].rearrange("p m t -> p (m t)")[:, 4 * CH * c : 4 * CH * (c + 1)].bitcast(I32),
+                in_=codes[:].bitcast(I32),
+            )
+            if un == 11 or un == 15:
+                plane = y_scales[0] if un == 11 else y_scales[1]
+                cols = slice(0, 3 * CH) if un == 11 else slice(3 * CH, 4 * CH)
+                for q in range(4):
+                    nc.sync.dma_start(
+                        out=out_2[:, 4 * q : 4 * q + 4, cols].rearrange("g r m -> r g m").bitcast(I32),
+                        in_=plane[32 * q : 32 * q + 4].bitcast(I32),
+                    )
+
+        def transpose_y(un):
+            y_out[un] = rot(work, "y_out", 5, [P, 2, 512], F32)
+            banks = []
+            for s in range(2):
+                bank = rot(psum, "ring", RING, [P, 4, P], F32)
+                banks.append(bank)
+                for t in range(4):
+                    nc.tensor.transpose(bank[:, t, :], y_t[un][:, t, P * s : P * (s + 1)], ident[:])
+            return banks
+
+        def copy_y(un, banks, s, on_vector):
+            dst = y_out[un][:, s, :].rearrange("m (p t) -> m p t", t=4)
+            src = banks[s][:].rearrange("m t p -> m p t")
+            move(on_vector, dst, src)
+
+        def store_y(un):
+            c, g = divmod(un, 4)
+            nc.sync.dma_start(
+                out=out_0[CH * c : CH * (c + 1), 512 * g : 512 * (g + 1)].rearrange("(s m) n -> m s n", m=P),
+                in_=y_out[un][:],
+            )
+
+        def spread_rows(col, row):
+            bank = rot(psum, "ring", RING, [P, 4, P], F32)
+            for t in range(4):
+                nc.tensor.transpose(bank[:, t, :], col[:, t : t + 1].to_broadcast([P, P]), ident[:])
+            nc.scalar.copy(
+                out=row[:].rearrange("m (u p e) -> m u p e", u=2, e=2),
+                in_=bank[:].rearrange("m (u e) p -> m u p e", e=2),
+            )
+
+        def permute_r(g):
+            nc.vector.tensor_copy(
+                out=r_words[g][:].rearrange("p t (m b) -> p t m b", b=2),
+                in_=r_raw[:, 1024 * g : 1024 * (g + 1)].rearrange("p (m t b) -> p t m b", t=4, b=2),
+            )
+
+        def permute_r_scales():
+            nc.vector.tensor_copy(
+                out=r_scales[:].rearrange("p (g t) m -> p g t m", t=4),
+                in_=rs_raw[:].rearrange("p (g m t) -> p g t m", g=4, t=4),
+            )
+
+        for s in range(HALVES + 1):
+            zi = (s - 4) // 2 if (s >= 4 and s % 2 == 0) else None
+            zc = (s - 3) // 2 if (s >= 3 and s % 2 == 1) else None
+            ub = s - 7
+            ua = s - 6
+            if zi is not None:
+                transpose_z(zi)
+            if s in (3, 4, 5):
+                quantise_x(s - 1)
+            if zc is not None:
+                centre_z(zc)
+            if s + 1 < HALVES and SPLIT[s + 1] == "a":
+                split_words(s + 1)
+            if s < HALVES:
+                banks_x = transpose_x(s)
+                copy_x(s, banks_x, 0, s == 0)
+                copy_x(s, banks_x, 1, s == 0)
+            if s == 0:
+                spread_rows(centre_col, centre_row)
+                spread_rows(inv_col, inv_row)
+            if s >= 6:
+                quantise_x(s - 1)
+            if s < 2:
+                quantise_x(s)
+            if zi is not None:
+                quantise_z(zi)
+            if ub >= 0:
+                interleave_y(ub)
+            if zc is not None:
+                scale_z(zc)
+            if ub >= 0:
+                banks_b = transpose_y(ub)
+                copy_y(ub, banks_b, 0, False)
+            if s + 1 < HALVES and SPLIT[s + 1] == "v":
+                split_words(s + 1)
+            if ub >= 0:
+                quantise_y(ub)
+                copy_y(ub, banks_b, 1, s % 2 == 0)
+                store_y(ub)
+            if s == 1:
+                permute_r_scales()
+            if s == 2:
+                nc.vector.tensor_copy(out=spread_col[:], in_=spread_raw[:].rearrange("p g t -> p (g t)"))
+                nc.vector.tensor_tensor(
+                    out=shift_col[:], in0=bias_raw[:].rearrange("p g t -> p (g t)"),
+                    in1=spread_raw[:].rearrange("p g t -> p (g t)"), op=ALU.mult,
+                )
+            if s in (3, 5, 6):
+                permute_r((3, 4, 5, 6).index(s))
+            if s == 4:
+                permute_r(1)
+            if s == HALVES:
+                stage1(s - 1)
+            if ua >= 0:
+                banks_a = stage2(ua)
+                affine(ua, banks_a, 0, False)
+                affine(ua, banks_a, 1, False)
+            if 1 <= s < HALVES:
+                stage1(s - 1)
+
+        last = M // P - 1
+        centre_z(last)
+        banks_a = stage2(11)
+        interleave_y(10)
+        scale_z(last)
+        affine(11, banks_a, 0, False)
+        banks_b = transpose_y(10)
+        transpose_z(last)
+        quantise_y(10)
+        affine(11, banks_a, 1, True)
+        quantise_z(last)
+        copy_y(10, banks_b, 0, False)
+        copy_y(10, banks_b, 1, False)
+        store_y(10)
+        for un in range(11, UNITS):
+            if un + 1 < UNITS:
+                banks_a = stage2(un + 1)
+            banks_b = transpose_y(un)
+            interleave_y(un)
+            if un + 1 < UNITS:
+                affine(un + 1, banks_a, 0, False)
+                affine(un + 1, banks_a, 1, True)
+            copy_y(un, banks_b, 0, False)
+            quantise_y(un)
+            copy_y(un, banks_b, 1, un + 1 == UNITS)
+            store_y(un)

@@ -18,11 +18,13 @@ ACT = mybir.ActivationFunctionType
 
 P = 128
 HALVES = 16
-UNITS = 16
 CH = 256
-SPLIT = "-------" + "v" * 9
+UNITS = [(c, g, 0, CH) for c in range(4) for g in range(4)]
+SPLIT = "-------a-v-v-v-v"
 X_BUFS = 16
 RING = 7
+XV = False
+AV = 2
 
 
 def tile_sst_pattern_rainfall_projection_h1_kernel(
@@ -73,13 +75,6 @@ def tile_sst_pattern_rainfall_projection_h1_kernel(
         nc.scalar.dma_start(out=inv_raw[:], in_=inv_scale.rearrange("(p t) -> p t", t=4))
         make_identity(nc, ident[:])
         nc.vector.memset(rs_raw[:].bitcast(I32), 0)
-        for q in range(4):
-            nc.gpsimd.dma_start(
-                out=rs_raw[32 * q : 32 * q + 4, :].bitcast(I32),
-                in_=regression_scales[0, 4 * q : 4 * q + 4, :].bitcast(I32),
-            )
-        nc.gpsimd.dma_start(out=spread_raw[:], in_=rain_spread.rearrange("(g p t) -> p g t", p=P, t=4))
-        nc.gpsimd.dma_start(out=bias_raw[:], in_=bias.rearrange("(g p t) -> p g t", p=P, t=4))
 
         x_raw = {}
 
@@ -102,19 +97,28 @@ def tile_sst_pattern_rainfall_projection_h1_kernel(
             )
         load_e(0)
         load_x(1)
-        load_e(1)
         load_x(2)
+        load_e(1)
         load_x(3)
+        for q in range(4):
+            nc.sync.dma_start(
+                out=rs_raw[32 * q : 32 * q + 4, :].bitcast(I32),
+                in_=regression_scales[0, 4 * q : 4 * q + 4, :].bitcast(I32),
+            )
+        load_x(4)
         nc.sync.dma_start(out=r_raw[:].bitcast(I32), in_=regression_words[0].bitcast(I32))
-        for h in range(4, HALVES):
+        load_x(5)
+        nc.sync.dma_start(out=spread_raw[:], in_=rain_spread.rearrange("(g p t) -> p g t", p=P, t=4))
+        nc.sync.dma_start(out=bias_raw[:], in_=bias.rearrange("(g p t) -> p g t", p=P, t=4))
+        for h in range(6, HALVES):
             load_x(h)
 
         nc.scalar.activation(out=centre_col[:], in_=centre_raw[:], func=ACT.Identity)
         nc.vector.tensor_copy(out=inv_col[:], in_=inv_raw[:])
 
         x_split, x_t, x_q = {}, {}, {}
-        acc, z_diff, z_bf, z_t, z_q = {}, {}, {}, {}, {}
-        y_t, y_bf, y_out = {}, {}, {}
+        acc, z_diff, z_bf, z_bank, z_t, z_q = {}, {}, {}, {}, {}, {}
+        y_t, y_bf, y_out, sums, turned, x_banks = {}, {}, {}, {}, {}, {}
 
         def move(on_vector, dst, src):
             if on_vector:
@@ -125,7 +129,7 @@ def tile_sst_pattern_rainfall_projection_h1_kernel(
         def split_words(h):
             if SPLIT[h] == "-":
                 return
-            x_split[h] = rot(work, "x_split", 2, [P, 2, 512], F32)
+            x_split[h] = rot(work, "x_split", 4, [P, 2, 512], F32)
             move(
                 SPLIT[h] == "v",
                 x_split[h][:].rearrange("m u (c i) -> m c u i", i=4),
@@ -133,7 +137,7 @@ def tile_sst_pattern_rainfall_projection_h1_kernel(
             )
 
         def transpose_x(h):
-            x_t[h] = rot(work, "x_t", 3, [P, 4, P, 2], F32)
+            x_t[h] = rot(work, "x_t", 4, [P, 4, P, 2], F32)
             banks = []
             for b in range(2):
                 bank = rot(psum, "ring", RING, [P, 2, 2, P], F32)
@@ -146,14 +150,14 @@ def tile_sst_pattern_rainfall_projection_h1_kernel(
                         else:
                             src = x_raw[h][:].bitcast(F32)[:, 256 * g + u : 256 * (g + 1) : 2]
                         nc.tensor.transpose(bank[:, gg, u, :], src, ident[:])
-            return banks
+            x_banks[h] = banks
 
-        def copy_x(h, banks, b, on_vector):
-            move(on_vector, x_t[h][:, 2 * b : 2 * b + 2], banks[b][:].rearrange("p g u m -> p g m u"))
+        def copy_x(h, b, on_vector):
+            move(on_vector, x_t[h][:, 2 * b : 2 * b + 2], x_banks[h][b][:].rearrange("p g u m -> p g m u"))
 
         def quantise_x(h):
-            codes = rot(work, "x_codes", 3, [P, 4 * P], U32)
-            scales = rot(work, "x_scales", 3, [P, 4 * P], U8)
+            codes = rot(work, "x_codes", 4, [P, 4 * P], U32)
+            scales = rot(work, "x_scales", 4, [P, 4 * P], U8)
             x_q[h] = (codes, scales)
             nc.vector.quantize_mx(
                 out=codes[:].bitcast(FP8X4),
@@ -193,10 +197,13 @@ def tile_sst_pattern_rainfall_projection_h1_kernel(
 
         def transpose_z(i):
             bank = rot(psum, "ring", RING, [P, 2, P], F32)
+            z_bank[i] = bank
             for u in range(2):
                 nc.tensor.transpose(bank[:, u, :], z_bf[i][:].bitcast(F32)[:, P * u : P * (u + 1)], ident[:])
+
+        def copy_z(i):
             z_t[i] = rot(work, "z_t", 2, [P, P, 2], F32)
-            nc.scalar.copy(out=z_t[i][:], in_=bank[:].rearrange("p u m -> p m u"))
+            nc.scalar.copy(out=z_t[i][:], in_=z_bank[i][:].rearrange("p u m -> p m u"))
 
         def quantise_z(i):
             c, s = divmod(i, 2)
@@ -210,92 +217,91 @@ def tile_sst_pattern_rainfall_projection_h1_kernel(
             )
 
         def stage2(un):
-            c, g = divmod(un, 4)
+            c, g, m0, w = UNITS[un]
             codes, scales = z_q[c]
-            banks = []
-            for b in range(2):
-                bank = rot(psum, "ring", RING, [P, 2, CH], F32)
-                banks.append(bank)
-                for tt in range(2):
-                    t = 2 * b + tt
-                    nc.tensor.matmul_mx(
-                        out=bank[:, tt, :],
-                        lhsT=r_words[g][:, t, :].bitcast(FP4X4),
-                        lhsT_scale=r_scales[:, 4 * g + t, :],
-                        rhs=codes[:].bitcast(FP8X4),
-                        rhs_scale=scales[:],
-                        start=True,
-                        stop=True,
-                    )
-            y_t[un] = rot(work, "y_t", 3, [P, 4, CH], F32)
-            return banks
+            per_bank = 512 // w
+            outs = []
+            for t in range(4):
+                if t % per_bank == 0:
+                    bank = rot(psum, "ring", RING, [P, per_bank, w], F32)
+                outs.append(bank[:, t % per_bank, :])
+                nc.tensor.matmul_mx(
+                    out=outs[t],
+                    lhsT=r_words[g][:, t, :].bitcast(FP4X4),
+                    lhsT_scale=r_scales[:, 4 * g + t, :],
+                    rhs=codes[:, m0 : m0 + w].bitcast(FP8X4),
+                    rhs_scale=scales[:, m0 : m0 + w],
+                    start=True,
+                    stop=True,
+                )
+            y_t[un] = rot(work, "y_t", 4, [P, 4, w], F32)
+            sums[un] = outs
 
-        def affine(un, banks, b, on_vector):
-            g = un % 4
-            for tt in range(2):
-                t = 2 * b + tt
-                col = slice(4 * g + t, 4 * g + t + 1)
-                if on_vector:
-                    nc.vector.tensor_scalar(
-                        out=y_t[un][:, t, :], in0=banks[b][:, tt, :], scalar1=spread_col[:, col],
-                        scalar2=shift_col[:, col], op0=ALU.mult, op1=ALU.add,
-                    )
-                else:
-                    nc.scalar.activation(
-                        out=y_t[un][:, t, :], in_=banks[b][:, tt, :], func=ACT.Identity,
-                        bias=shift_col[:, col], scale=spread_col[:, col],
-                    )
+        def affine(un, t, on_vector):
+            g = UNITS[un][1]
+            col = slice(4 * g + t, 4 * g + t + 1)
+            if on_vector:
+                nc.vector.tensor_scalar(
+                    out=y_t[un][:, t, :], in0=sums[un][t], scalar1=spread_col[:, col],
+                    scalar2=shift_col[:, col], op0=ALU.mult, op1=ALU.add,
+                )
+            else:
+                nc.scalar.activation(
+                    out=y_t[un][:, t, :], in_=sums[un][t], func=ACT.Identity,
+                    bias=shift_col[:, col], scale=spread_col[:, col],
+                )
 
         def interleave_y(un):
-            y_bf[un] = rot(work, "y_bf", 2, [P, CH, 4], BF16)
+            y_bf[un] = rot(work, "y_bf", 3, [P, UNITS[un][3], 4], BF16)
             nc.vector.tensor_copy(
                 out=y_bf[un][:].rearrange("p (c i) t -> p c t i", i=4),
                 in_=y_t[un][:].rearrange("p t (c i) -> p c t i", i=4),
             )
 
         def quantise_y(un):
-            c, g = divmod(un, 4)
-            codes = rot(work, "y_codes", 4, [P, CH], U32)
-            if c < 3:
-                scales = y_scales[0][:, g, CH * c : CH * (c + 1)]
-            else:
-                scales = y_scales[1][:, g, :]
+            c, g, m0, w = UNITS[un]
+            codes = rot(work, "y_codes", 4, [P, w], U32)
             nc.vector.quantize_mx(
-                out=codes[:].bitcast(FP8X4), scales=scales, in_=y_bf[un][:].rearrange("p m t -> p (m t)")
+                out=codes[:].bitcast(FP8X4),
+                scales=y_scales[c // 3][:, g, CH * (c % 3) + m0 : CH * (c % 3) + m0 + w],
+                in_=y_bf[un][:].rearrange("p m t -> p (m t)"),
             )
+            first = CH * c + m0
             nc.sync.dma_start(
-                out=out_1[g].rearrange("p m t -> p (m t)")[:, 4 * CH * c : 4 * CH * (c + 1)].bitcast(I32),
+                out=out_1[g].rearrange("p m t -> p (m t)")[:, 4 * first : 4 * (first + w)].bitcast(I32),
                 in_=codes[:].bitcast(I32),
             )
-            if un == 11 or un == 15:
-                plane = y_scales[0] if un == 11 else y_scales[1]
-                cols = slice(0, 3 * CH) if un == 11 else slice(3 * CH, 4 * CH)
+            if g == 3 and c >= 2:
+                cols = slice(0, 3 * CH) if c == 2 else slice(3 * CH, 4 * CH)
                 for q in range(4):
                     nc.sync.dma_start(
                         out=out_2[:, 4 * q : 4 * q + 4, cols].rearrange("g r m -> r g m").bitcast(I32),
-                        in_=plane[32 * q : 32 * q + 4].bitcast(I32),
+                        in_=y_scales[c // 3][32 * q : 32 * q + 4].bitcast(I32),
                     )
 
         def transpose_y(un):
-            y_out[un] = rot(work, "y_out", 5, [P, 2, 512], F32)
-            banks = []
-            for s in range(2):
+            w = UNITS[un][3]
+            y_out[un] = rot(work, "y_out", 5, [P, w // P, 512], F32)
+            turned[un] = []
+            for s in range(w // P):
                 bank = rot(psum, "ring", RING, [P, 4, P], F32)
-                banks.append(bank)
+                turned[un].append(bank)
                 for t in range(4):
                     nc.tensor.transpose(bank[:, t, :], y_t[un][:, t, P * s : P * (s + 1)], ident[:])
-            return banks
 
-        def copy_y(un, banks, s, on_vector):
-            dst = y_out[un][:, s, :].rearrange("m (p t) -> m p t", t=4)
-            src = banks[s][:].rearrange("m t p -> m p t")
-            move(on_vector, dst, src)
+        def copy_y(un, s, on_vector):
+            move(
+                on_vector,
+                y_out[un][:, s, :].rearrange("m (p t) -> m p t", t=4),
+                turned[un][s][:].rearrange("m t p -> m p t"),
+            )
 
-        def store_y(un):
-            c, g = divmod(un, 4)
+        def store_y(un, s0, count):
+            c, g, m0, w = UNITS[un]
+            first = CH * c + m0 + P * s0
             nc.sync.dma_start(
-                out=out_0[CH * c : CH * (c + 1), 512 * g : 512 * (g + 1)].rearrange("(s m) n -> m s n", m=P),
-                in_=y_out[un][:],
+                out=out_0[first : first + P * count, 512 * g : 512 * (g + 1)].rearrange("(s m) n -> m s n", m=P),
+                in_=y_out[un][:, s0 : s0 + count, :],
             )
 
         def spread_rows(col, row):
@@ -319,89 +325,153 @@ def tile_sst_pattern_rainfall_projection_h1_kernel(
                 in_=rs_raw[:].rearrange("p (g m t) -> p g t m", g=4, t=4),
             )
 
-        for s in range(HALVES + 1):
-            zi = (s - 4) // 2 if (s >= 4 and s % 2 == 0) else None
-            zc = (s - 3) // 2 if (s >= 3 and s % 2 == 1) else None
-            ub = s - 7
-            ua = s - 6
-            if zi is not None:
-                transpose_z(zi)
-            if s in (3, 4, 5):
-                quantise_x(s - 1)
-            if zc is not None:
-                centre_z(zc)
-            if s + 1 < HALVES and SPLIT[s + 1] == "a":
-                split_words(s + 1)
-            if s < HALVES:
-                banks_x = transpose_x(s)
-                copy_x(s, banks_x, 0, s == 0)
-                copy_x(s, banks_x, 1, s == 0)
-            if s == 0:
-                spread_rows(centre_col, centre_row)
-                spread_rows(inv_col, inv_row)
-            if s >= 6:
-                quantise_x(s - 1)
-            if s < 2:
-                quantise_x(s)
-            if zi is not None:
-                quantise_z(zi)
-            if ub >= 0:
-                interleave_y(ub)
-            if zc is not None:
-                scale_z(zc)
-            if ub >= 0:
-                banks_b = transpose_y(ub)
-                copy_y(ub, banks_b, 0, False)
-            if s + 1 < HALVES and SPLIT[s + 1] == "v":
-                split_words(s + 1)
-            if ub >= 0:
-                quantise_y(ub)
-                copy_y(ub, banks_b, 1, s % 2 == 0)
-                store_y(ub)
-            if s == 1:
-                permute_r_scales()
-            if s == 2:
+        transpose_x(0)
+        copy_x(0, 0, True)
+        copy_x(0, 1, True)
+        spread_rows(centre_col, centre_row)
+        spread_rows(inv_col, inv_row)
+        quantise_x(0)
+        transpose_x(1)
+        copy_x(1, 0, False)
+        copy_x(1, 1, False)
+        stage1(0)
+        quantise_x(1)
+        transpose_x(2)
+        copy_x(2, 0, False)
+        copy_x(2, 1, False)
+        stage1(1)
+        permute_r_scales()
+        quantise_x(2)
+        centre_z(0)
+        transpose_x(3)
+        copy_x(3, 0, False)
+        copy_x(3, 1, False)
+        stage1(2)
+        scale_z(0)
+        quantise_x(3)
+        split_words(4)
+        split_words(5)
+        permute_r(0)
+        permute_r(1)
+        for i in range(2, 8):
+            a0, a1 = 2 * (i - 3), 2 * (i - 3) + 1
+            b0, b1 = a0 - 2, a1 - 2
+            ha, hb = 2 * i, 2 * i + 1
+            zi = i - 2
+            if i > 2:
+                centre_z(zi)
+            transpose_x(ha)
+            copy_x(ha, 0, False)
+            copy_x(ha, 1, False)
+            transpose_x(hb)
+            copy_x(hb, 0, False)
+            if b0 >= 0:
+                interleave_y(b0)
+            if i > 2:
+                scale_z(zi)
+            if i == 4:
+                permute_r(3)
+            copy_x(hb, 1, XV and i > 3)
+            quantise_x(ha)
+            if b0 >= 0:
+                transpose_y(b0)
+                transpose_y(b1)
+            transpose_z(zi)
+            if b0 >= 0:
+                copy_y(b0, 0, False)
+                quantise_y(b0)
+                interleave_y(b1)
+            copy_z(zi)
+            if b0 >= 0:
+                copy_y(b0, 1, True)
+                store_y(b0, 0, 2)
+            quantise_z(zi)
+            if b0 >= 0:
+                copy_y(b1, 0, False)
+                copy_y(b1, 1, False)
+                store_y(b1, 0, 2)
+            quantise_x(hb)
+            if b0 >= 0:
+                quantise_y(b1)
+            if i == 2:
                 nc.vector.tensor_copy(out=spread_col[:], in_=spread_raw[:].rearrange("p g t -> p (g t)"))
                 nc.vector.tensor_tensor(
                     out=shift_col[:], in0=bias_raw[:].rearrange("p g t -> p (g t)"),
                     in1=spread_raw[:].rearrange("p g t -> p (g t)"), op=ALU.mult,
                 )
-            if s in (3, 5, 6):
-                permute_r((3, 4, 5, 6).index(s))
-            if s == 4:
-                permute_r(1)
-            if s == HALVES:
-                stage1(s - 1)
-            if ua >= 0:
-                banks_a = stage2(ua)
-                affine(ua, banks_a, 0, False)
-                affine(ua, banks_a, 1, False)
-            if 1 <= s < HALVES:
-                stage1(s - 1)
+            if i < 7:
+                split_words(ha + 2)
+                split_words(hb + 2)
+            if i == 3:
+                permute_r(2)
+            if i > 2:
+                stage1(ha - 2)
+            if a0 >= 0:
+                stage2(a0)
+                stage2(a1)
+            stage1(hb - 2)
+            if a0 >= 0:
+                for t in range(4):
+                    affine(a0, t, False)
+                for t in range(4):
+                    affine(a1, t, t >= AV)
 
-        last = M // P - 1
-        centre_z(last)
-        banks_a = stage2(11)
+        centre_z(6)
+        transpose_y(8)
+        interleave_y(8)
+        copy_y(8, 0, False)
+        scale_z(6)
+        transpose_y(9)
+        copy_y(8, 1, False)
+        store_y(8, 0, 2)
+        stage2(10)
+        stage1(14)
+        stage1(15)
+        quantise_y(8)
+        interleave_y(9)
+        copy_y(9, 0, False)
+        copy_y(9, 1, False)
+        store_y(9, 0, 2)
+        affine(10, 2, True)
+        affine(10, 3, True)
+        affine(10, 0, False)
+        affine(10, 1, False)
+        quantise_y(9)
+        stage2(11)
+        centre_z(7)
+        transpose_z(6)
+        transpose_y(10)
+        affine(11, 0, False)
+        affine(11, 1, False)
         interleave_y(10)
-        scale_z(last)
-        affine(11, banks_a, 0, False)
-        banks_b = transpose_y(10)
-        transpose_z(last)
+        scale_z(7)
+        transpose_z(7)
+        copy_z(6)
+        affine(11, 2, False)
+        copy_z(7)
+        quantise_z(6)
+        affine(11, 3, True)
+        quantise_z(7)
+        copy_y(10, 0, False)
         quantise_y(10)
-        affine(11, banks_a, 1, True)
-        quantise_z(last)
-        copy_y(10, banks_b, 0, False)
-        copy_y(10, banks_b, 1, False)
-        store_y(10)
-        for un in range(11, UNITS):
-            if un + 1 < UNITS:
-                banks_a = stage2(un + 1)
-            banks_b = transpose_y(un)
+        copy_y(10, 1, True)
+        store_y(10, 0, 2)
+        last = len(UNITS) - 1
+        for un in range(11, last + 1):
+            if un < last:
+                stage2(un + 1)
+            transpose_y(un)
             interleave_y(un)
-            if un + 1 < UNITS:
-                affine(un + 1, banks_a, 0, False)
-                affine(un + 1, banks_a, 1, True)
-            copy_y(un, banks_b, 0, False)
-            quantise_y(un)
-            copy_y(un, banks_b, 1, un + 1 == UNITS)
-            store_y(un)
+            if un < last:
+                for t in range(4):
+                    affine(un + 1, t, t >= 2)
+            copy_y(un, 0, False)
+            if un < last:
+                quantise_y(un)
+                copy_y(un, 1, False)
+                store_y(un, 0, 2)
+            else:
+                store_y(un, 0, 1)
+                copy_y(un, 1, True)
+                store_y(un, 1, 1)
+                quantise_y(un)

@@ -20,11 +20,11 @@ P = 128
 HALVES = 16
 CH = 256
 UNITS = [(c, g, 0, CH) for c in range(4) for g in range(4)]
-SPLIT = "-------a-v-v-v-v"
-X_BUFS = 16
+SPLIT = "----av-avvvvvvvv"
+X_BUFS = 6
 RING = 7
 XV = False
-AV = 2
+AV = 4
 
 
 def tile_sst_pattern_rainfall_projection_h1_kernel(
@@ -83,6 +83,12 @@ def tile_sst_pattern_rainfall_projection_h1_kernel(
             x_raw[h] = rot(work, "x_raw", X_BUFS, [P, 2048], BF16)
             nc.sync.dma_start(out=x_raw[h][:], in_=sst[P * i : P * (i + 1), 2048 * j : 2048 * (j + 1)])
 
+        def load_x_tile(i):
+            both = rot(work, "x_tile", 5, [P, 4096], BF16)
+            nc.sync.dma_start(out=both[:], in_=sst[P * i : P * (i + 1), :])
+            x_raw[2 * i] = both[:, :2048]
+            x_raw[2 * i + 1] = both[:, 2048:]
+
         def load_e(j):
             nc.sync.dma_start(
                 out=e_words[j][:].bitcast(I32),
@@ -110,15 +116,15 @@ def tile_sst_pattern_rainfall_projection_h1_kernel(
         load_x(5)
         nc.sync.dma_start(out=spread_raw[:], in_=rain_spread.rearrange("(g p t) -> p g t", p=P, t=4))
         nc.sync.dma_start(out=bias_raw[:], in_=bias.rearrange("(g p t) -> p g t", p=P, t=4))
-        for h in range(6, HALVES):
-            load_x(h)
+        for i in range(3, M // P):
+            load_x_tile(i)
 
         nc.scalar.activation(out=centre_col[:], in_=centre_raw[:], func=ACT.Identity)
         nc.vector.tensor_copy(out=inv_col[:], in_=inv_raw[:])
 
         x_split, x_t, x_q = {}, {}, {}
         acc, z_diff, z_bf, z_bank, z_t, z_q = {}, {}, {}, {}, {}, {}
-        y_t, y_bf, y_out, sums, turned, x_banks = {}, {}, {}, {}, {}, {}
+        y_t, y_bf, y_out, y_pair, sums, turned, x_banks = {}, {}, {}, {}, {}, {}, {}
 
         def move(on_vector, dst, src):
             if on_vector:
@@ -253,10 +259,7 @@ def tile_sst_pattern_rainfall_projection_h1_kernel(
 
         def interleave_y(un):
             y_bf[un] = rot(work, "y_bf", 3, [P, UNITS[un][3], 4], BF16)
-            nc.vector.tensor_copy(
-                out=y_bf[un][:].rearrange("p (c i) t -> p c t i", i=4),
-                in_=y_t[un][:].rearrange("p t (c i) -> p c t i", i=4),
-            )
+            nc.vector.tensor_copy(out=y_bf[un][:], in_=y_t[un][:].rearrange("p t m -> p m t"))
 
         def quantise_y(un):
             c, g, m0, w = UNITS[un]
@@ -281,7 +284,12 @@ def tile_sst_pattern_rainfall_projection_h1_kernel(
 
         def transpose_y(un):
             w = UNITS[un][3]
-            y_out[un] = rot(work, "y_out", 5, [P, w // P, 512], F32)
+            if un >= 8:
+                y_out[un] = rot(work, "y_out", 4, [P, w // P, 512], F32)
+            else:
+                if un % 2 == 0:
+                    y_pair[un // 2] = rot(work, "y_pair", 2, [P, w // P, 1024], F32)
+                y_out[un] = y_pair[un // 2][:, :, 512 * (un % 2) : 512 * (un % 2 + 1)]
             turned[un] = []
             for s in range(w // P):
                 bank = rot(psum, "ring", RING, [P, 4, P], F32)
@@ -302,6 +310,13 @@ def tile_sst_pattern_rainfall_projection_h1_kernel(
             nc.sync.dma_start(
                 out=out_0[first : first + P * count, 512 * g : 512 * (g + 1)].rearrange("(s m) n -> m s n", m=P),
                 in_=y_out[un][:, s0 : s0 + count, :],
+            )
+
+        def store_y_pair(un):
+            c, g, m0, w = UNITS[un]
+            nc.sync.dma_start(
+                out=out_0[CH * c : CH * (c + 1), 512 * g : 512 * (g + 2)].rearrange("(s m) n -> m s n", m=P),
+                in_=y_pair[un // 2][:],
             )
 
         def spread_rows(col, row):
@@ -339,17 +354,18 @@ def tile_sst_pattern_rainfall_projection_h1_kernel(
         transpose_x(2)
         copy_x(2, 0, False)
         copy_x(2, 1, False)
+        split_words(3)
         stage1(1)
         permute_r_scales()
         quantise_x(2)
         centre_z(0)
         transpose_x(3)
+        split_words(4)
         copy_x(3, 0, False)
         copy_x(3, 1, False)
         stage1(2)
         scale_z(0)
         quantise_x(3)
-        split_words(4)
         split_words(5)
         permute_r(0)
         permute_r(1)
@@ -384,12 +400,11 @@ def tile_sst_pattern_rainfall_projection_h1_kernel(
             copy_z(zi)
             if b0 >= 0:
                 copy_y(b0, 1, True)
-                store_y(b0, 0, 2)
             quantise_z(zi)
             if b0 >= 0:
                 copy_y(b1, 0, False)
                 copy_y(b1, 1, False)
-                store_y(b1, 0, 2)
+                store_y_pair(b0)
             quantise_x(hb)
             if b0 >= 0:
                 quantise_y(b1)

@@ -17,14 +17,24 @@ ALU = mybir.AluOpType
 ACT = mybir.ActivationFunctionType
 
 P = 128
-HALVES = 16
-CH = 256
-UNITS = [(c, g, 0, CH) for c in range(4) for g in range(4)]
-SPLIT = "----av-avvvvvvvv"
-X_BUFS = 6
+PACK = 4
+GROUP = P * PACK
+HALF = C // 2
+CHUNK = 2 * P
+TILES = M // P
+HALVES = 2 * TILES
+RAIN_GROUPS = N // GROUP
+UNITS = (M // CHUNK) * RAIN_GROUPS
 RING = 7
-XV = False
-AV = 4
+FINE_TILES = 4
+PAIRED_UNITS = 8
+
+GATHER_ON_SCALAR = (5, 7, 9)
+GATHER_ON_VECTOR = range(10, HALVES)
+
+SPREAD_ROW, BIAS_ROW, CENTRE_ROW, INV_ROW, VECTOR_ROWS = 0, 4, 8, 9, 10
+
+ON_VECTOR, ON_SCALAR = True, False
 
 
 def tile_sst_pattern_rainfall_projection_h1_kernel(
@@ -38,93 +48,112 @@ def tile_sst_pattern_rainfall_projection_h1_kernel(
         psum = ctx.enter_context(tc.psum_pool(name="psum", bufs=1))
         ctx.enter_context(tc.manual_schedule())
 
-        counts = {}
+        uses = {}
 
-        def rot(pool, tag, depth, shape, dtype):
-            k = counts.get(tag, 0)
-            counts[tag] = k + 1
-            slot = "%s%d" % (tag, k % depth)
-            if pool is psum:
-                return pool.tile(shape, dtype, name=slot, tag=slot)
-            return pool.tile(shape, dtype, name=slot, tag=slot, align_bytes=64)
+        def next_slot(kind, depth):
+            count = uses.get(kind, 0)
+            uses[kind] = count + 1
+            return "%s%d" % (kind, count % depth)
+
+        def buffer(kind, depth, shape, dtype):
+            slot = next_slot(kind, depth)
+            return work.tile(shape, dtype, name=slot, tag=slot, align_bytes=64)
+
+        def bank(kind, depth, shape, dtype):
+            slot = next_slot(kind, depth)
+            return psum.tile(shape, dtype, name=slot, tag=slot)
 
         ident = keep.tile([P, P], F32, align_bytes=64)
+        ident_bf = keep.tile([P, P], BF16, align_bytes=64)
         e_words = [keep.tile([P, 4, 2 * F], U8, name="e_words%d" % j, align_bytes=64) for j in range(2)]
-        e_scales = keep.tile([P, 8, F], U8, align_bytes=64)
-        r_raw = keep.tile([P, 2 * N], U8, align_bytes=64)
-        rs_raw = keep.tile([P, N], U8, align_bytes=64)
-        r_words = [keep.tile([P, 4, 2 * P], U8, name="r_words%d" % g, align_bytes=64) for g in range(4)]
-        r_scales = keep.tile([P, 16, P], U8, align_bytes=64)
-        centre_raw = keep.tile([P, 4], BF16, align_bytes=64)
-        inv_raw = keep.tile([P, 4], BF16, align_bytes=64)
-        bias_raw = keep.tile([P, 4, 4], BF16, align_bytes=64)
-        spread_raw = keep.tile([P, 4, 4], BF16, align_bytes=64)
-        centre_col = keep.tile([P, 4], F32, align_bytes=64)
-        inv_col = keep.tile([P, 4], F32, align_bytes=64)
-        spread_col = keep.tile([P, 16], F32, align_bytes=64)
-        shift_col = keep.tile([P, 16], F32, align_bytes=64)
+        e_scales = [keep.tile([P, 4, F], U8, name="e_scales%d" % j, align_bytes=64) for j in range(2)]
+        r_loaded = [keep.tile([P, N], U8, name="r_loaded%d" % j, align_bytes=64) for j in range(2)]
+        r_scales_loaded = keep.tile([P, N], U8, align_bytes=64)
+        r_words = [keep.tile([P, PACK, 2 * P], U8, name="r_words%d" % g, align_bytes=64) for g in range(RAIN_GROUPS)]
+        r_scales = keep.tile([P, RAIN_GROUPS * PACK, P], U8, name="r_scales", align_bytes=64)
+        vector_rows = keep.tile([P, GROUP], BF16, align_bytes=64)
+        vector_cols = keep.tile([P, VECTOR_ROWS, PACK], F32, align_bytes=64)
+        spread_col = vector_cols[:, SPREAD_ROW:BIAS_ROW, :].rearrange("p g t -> p (g t)")
+        shift_col = keep.tile([P, RAIN_GROUPS * PACK], F32, align_bytes=64)
         centre_row = keep.tile([P, F], F32, align_bytes=64)
         inv_row = keep.tile([P, F], F32, align_bytes=64)
         y_scales = [
-            keep.tile([P, 4, 3 * CH], U8, name="y_scales0", align_bytes=64),
-            keep.tile([P, 4, CH], U8, name="y_scales1", align_bytes=64),
+            keep.tile([P, RAIN_GROUPS, CHUNK], U8, name="y_scales%d" % c, align_bytes=64) for c in range(M // CHUNK)
         ]
 
-        nc.vector.memset(e_scales[:].rearrange("p g n -> p (g n)").bitcast(I32), 0)
-        nc.scalar.dma_start(out=centre_raw[:], in_=centre.rearrange("(p t) -> p t", t=4))
-        nc.scalar.dma_start(out=inv_raw[:], in_=inv_scale.rearrange("(p t) -> p t", t=4))
+        nc.vector.memset(vector_rows[:], 0.0)
+        nc.vector.memset(e_scales[0][:].rearrange("p g n -> p (g n)").bitcast(I32), 0)
+        nc.vector.memset(e_scales[1][:].rearrange("p g n -> p (g n)").bitcast(I32), 0)
+        nc.vector.memset(r_scales_loaded[:].bitcast(I32), 0)
         make_identity(nc, ident[:])
-        nc.vector.memset(rs_raw[:].bitcast(I32), 0)
+        nc.scalar.activation(out=ident_bf[:], in_=ident[:], func=ACT.Identity)
 
         x_raw = {}
 
-        def load_x(h):
+        def load_half(h):
             i, j = divmod(h, 2)
-            x_raw[h] = rot(work, "x_raw", X_BUFS, [P, 2048], BF16)
-            nc.sync.dma_start(out=x_raw[h][:], in_=sst[P * i : P * (i + 1), 2048 * j : 2048 * (j + 1)])
+            x_raw[h] = buffer("x_raw", 2 * FINE_TILES, [P, HALF], BF16)
+            nc.sync.dma_start(out=x_raw[h][:], in_=sst[P * i : P * (i + 1), HALF * j : HALF * (j + 1)])
 
-        def load_x_tile(i):
-            both = rot(work, "x_tile", 5, [P, 4096], BF16)
+        def load_tile(i):
+            both = buffer("x_tile", TILES - FINE_TILES, [P, C], BF16)
             nc.sync.dma_start(out=both[:], in_=sst[P * i : P * (i + 1), :])
-            x_raw[2 * i] = both[:, :2048]
-            x_raw[2 * i + 1] = both[:, 2048:]
+            x_raw[2 * i] = both[:, :HALF]
+            x_raw[2 * i + 1] = both[:, HALF:]
 
-        def load_e(j):
+        def load_e_words(j):
             nc.sync.dma_start(
                 out=e_words[j][:].bitcast(I32),
                 in_=patterns_words[4 * j : 4 * j + 4].rearrange("g p n -> p g n").bitcast(I32),
             )
 
-        load_x(0)
-        for q in range(4):
-            nc.sync.dma_start(
-                out=e_scales[32 * q : 32 * q + 4].bitcast(I32),
-                in_=patterns_scales[:, 4 * q : 4 * q + 4, :].rearrange("g r n -> r g n").bitcast(I32),
-            )
-        load_e(0)
-        load_x(1)
-        load_x(2)
-        load_e(1)
-        load_x(3)
-        for q in range(4):
-            nc.sync.dma_start(
-                out=rs_raw[32 * q : 32 * q + 4, :].bitcast(I32),
-                in_=regression_scales[0, 4 * q : 4 * q + 4, :].bitcast(I32),
-            )
-        load_x(4)
-        nc.sync.dma_start(out=r_raw[:].bitcast(I32), in_=regression_words[0].bitcast(I32))
-        load_x(5)
-        nc.sync.dma_start(out=spread_raw[:], in_=rain_spread.rearrange("(g p t) -> p g t", p=P, t=4))
-        nc.sync.dma_start(out=bias_raw[:], in_=bias.rearrange("(g p t) -> p g t", p=P, t=4))
-        for i in range(3, M // P):
-            load_x_tile(i)
+        def load_e_scales(j):
+            for q in range(4):
+                rows = patterns_scales[4 * j : 4 * j + 4, 4 * q : 4 * q + 4, :]
+                nc.sync.dma_start(
+                    out=e_scales[j][32 * q : 32 * q + 4].bitcast(I32),
+                    in_=rows.rearrange("g r n -> r g n").bitcast(I32),
+                )
 
-        nc.scalar.activation(out=centre_col[:], in_=centre_raw[:], func=ACT.Identity)
-        nc.vector.tensor_copy(out=inv_col[:], in_=inv_raw[:])
+        def load_r_scales():
+            for q in range(4):
+                nc.sync.dma_start(
+                    out=r_scales_loaded[32 * q : 32 * q + 4, :].bitcast(I32),
+                    in_=regression_scales[0, 4 * q : 4 * q + 4, :].bitcast(I32),
+                )
 
-        x_split, x_t, x_q = {}, {}, {}
-        acc, z_diff, z_bf, z_bank, z_t, z_q = {}, {}, {}, {}, {}, {}
-        y_t, y_bf, y_out, y_pair, sums, turned, x_banks = {}, {}, {}, {}, {}, {}, {}
+        def load_r_words(j):
+            nc.sync.dma_start(
+                out=r_loaded[j][:].bitcast(I32), in_=regression_words[0, :, N * j : N * (j + 1)].bitcast(I32)
+            )
+
+        def load_vectors():
+            for row, vec, rows in (
+                (SPREAD_ROW, rain_spread, RAIN_GROUPS),
+                (BIAS_ROW, bias, RAIN_GROUPS),
+                (CENTRE_ROW, centre, 1),
+                (INV_ROW, inv_scale, 1),
+            ):
+                nc.sync.dma_start(out=vector_rows[row : row + rows, :], in_=vec.rearrange("(g n) -> g n", g=rows))
+
+        load_half(0)
+        load_vectors()
+        load_half(1)
+        load_e_scales(0)
+        load_e_words(0)
+        load_r_scales()
+        load_half(2)
+        load_e_scales(1)
+        load_e_words(1)
+        load_half(3)
+        load_r_words(0)
+        load_half(4)
+        load_half(5)
+        load_r_words(1)
+        load_half(6)
+        load_half(7)
+        for i in range(FINE_TILES, TILES):
+            load_tile(i)
 
         def move(on_vector, dst, src):
             if on_vector:
@@ -132,64 +161,100 @@ def tile_sst_pattern_rainfall_projection_h1_kernel(
             else:
                 nc.scalar.copy(out=dst, in_=src)
 
-        def split_words(h):
-            if SPLIT[h] == "-":
-                return
-            x_split[h] = rot(work, "x_split", 4, [P, 2, 512], F32)
-            move(
-                SPLIT[h] == "v",
-                x_split[h][:].rearrange("m u (c i) -> m c u i", i=4),
-                x_raw[h][:].bitcast(F32).rearrange("m (c i u) -> m c u i", i=4, u=2),
+        def turn_vectors():
+            turned_rows = bank("ring", RING, [P, PACK, P], BF16)
+            for t in range(PACK):
+                nc.tensor.transpose(turned_rows[:, t, :], vector_rows[:, t:GROUP:PACK], ident_bf[:])
+            nc.vector.tensor_copy(
+                out=vector_cols[:], in_=turned_rows[:, :, 0:VECTOR_ROWS].rearrange("p t r -> p r t")
+            )
+            nc.vector.tensor_tensor(
+                out=shift_col[:],
+                in0=vector_cols[:, BIAS_ROW:CENTRE_ROW, :].rearrange("p g t -> p (g t)"),
+                in1=spread_col,
+                op=ALU.mult,
             )
 
+        def repeat_on_partitions(r, row):
+            repeated = bank("ring", RING, [P, PACK, P], F32)
+            for t in range(PACK):
+                nc.tensor.transpose(repeated[:, t, :], vector_cols[:, r, t : t + 1].to_broadcast([P, P]), ident[:])
+            nc.scalar.copy(
+                out=row[:].rearrange("m (u p e) -> m u p e", u=2, e=2),
+                in_=repeated[:].rearrange("m (u e) p -> m u p e", e=2),
+            )
+
+        def reorder_r_words(g):
+            loaded = r_loaded[g // 2][:, 2 * GROUP * (g % 2) : 2 * GROUP * (g % 2 + 1)]
+            nc.vector.tensor_copy(
+                out=r_words[g][:].rearrange("k t (p b) -> k t p b", b=2),
+                in_=loaded.rearrange("k (p t b) -> k t p b", t=PACK, b=2),
+            )
+
+        def reorder_r_scales():
+            nc.vector.tensor_copy(
+                out=r_scales[:].rearrange("k (g t) p -> k g t p", t=PACK),
+                in_=r_scales_loaded[:].rearrange("k (g p t) -> k g t p", g=RAIN_GROUPS, t=PACK),
+            )
+
+        x_gathered, x_banks, x_turned, x_quant = {}, {}, {}, {}
+        acc, z_diff, z_bf, z_bank, z_turned, z_quant = {}, {}, {}, {}, {}, {}
+
+        def gather_pairs(h):
+            if h in GATHER_ON_VECTOR or h in GATHER_ON_SCALAR:
+                x_gathered[h] = buffer("x_gathered", 4, [P, 2, HALF // 4], F32)
+                move(
+                    h in GATHER_ON_VECTOR,
+                    x_gathered[h][:].rearrange("m u (c i) -> m c u i", i=4),
+                    x_raw[h][:].bitcast(F32).rearrange("m (c i u) -> m c u i", i=4, u=2),
+                )
+
         def transpose_x(h):
-            x_t[h] = rot(work, "x_t", 4, [P, 4, P, 2], F32)
-            banks = []
+            x_turned[h] = buffer("x_turned", 4, [P, 4, P, 2], F32)
+            x_banks[h] = []
             for b in range(2):
-                bank = rot(psum, "ring", RING, [P, 2, 2, P], F32)
-                banks.append(bank)
+                turned = bank("ring", RING, [P, 2, 2, P], F32)
+                x_banks[h].append(turned)
                 for gg in range(2):
                     g = 2 * b + gg
                     for u in range(2):
-                        if SPLIT[h] != "-":
-                            src = x_split[h][:, u, P * g : P * (g + 1)]
+                        if h in x_gathered:
+                            pairs = x_gathered[h][:, u, P * g : P * (g + 1)]
                         else:
-                            src = x_raw[h][:].bitcast(F32)[:, 256 * g + u : 256 * (g + 1) : 2]
-                        nc.tensor.transpose(bank[:, gg, u, :], src, ident[:])
-            x_banks[h] = banks
+                            pairs = x_raw[h][:].bitcast(F32)[:, 2 * P * g + u : 2 * P * (g + 1) : 2]
+                        nc.tensor.transpose(turned[:, gg, u, :], pairs, ident[:])
 
         def copy_x(h, b, on_vector):
-            move(on_vector, x_t[h][:, 2 * b : 2 * b + 2], x_banks[h][b][:].rearrange("p g u m -> p g m u"))
+            move(on_vector, x_turned[h][:, 2 * b : 2 * b + 2], x_banks[h][b][:].rearrange("p g u m -> p g m u"))
 
         def quantise_x(h):
-            codes = rot(work, "x_codes", 4, [P, 4 * P], U32)
-            scales = rot(work, "x_scales", 4, [P, 4 * P], U8)
-            x_q[h] = (codes, scales)
+            codes = buffer("x_codes", 4, [P, 4 * P], U32)
+            scales = buffer("x_scales", 4, [P, 4 * P], U8)
+            x_quant[h] = (codes, scales)
             nc.vector.quantize_mx(
                 out=codes[:].bitcast(FP8X4),
                 scales=scales[:],
-                in_=x_t[h][:].rearrange("p g m u -> p (g m u)").bitcast(BF16),
+                in_=x_turned[h][:].rearrange("p g m u -> p (g m u)").bitcast(BF16),
             )
 
         def stage1(h):
             i, j = divmod(h, 2)
             if j == 0:
-                acc[i] = rot(psum, "acc", 1, [P, F], F32)
-            codes, scales = x_q[h]
+                acc[i] = bank("acc", 1, [P, F], F32)
+            codes, scales = x_quant[h]
             for gg in range(4):
-                g = 4 * j + gg
                 nc.tensor.matmul_mx(
                     out=acc[i][:],
                     lhsT=codes[:, P * gg : P * (gg + 1)].bitcast(FP8X4),
                     lhsT_scale=scales[:, P * gg : P * (gg + 1)],
                     rhs=e_words[j][:, gg, :].bitcast(FP4X4),
-                    rhs_scale=e_scales[:, g, :],
-                    start=(g == 0),
-                    stop=(g == 7),
+                    rhs_scale=e_scales[j][:, gg, :],
+                    start=(j == 0 and gg == 0),
+                    stop=(j == 1 and gg == 3),
                 )
 
         def centre_z(i):
-            z_diff[i] = rot(work, "z_diff", 1, [P, F], F32)
+            z_diff[i] = buffer("z_diff", 1, [P, F], F32)
             nc.vector.tensor_tensor(
                 out=z_diff[i][:].rearrange("m (u p e) -> m u p e", u=2, e=2),
                 in0=acc[i][:].rearrange("m (p u e) -> m u p e", u=2, e=2),
@@ -198,295 +263,262 @@ def tile_sst_pattern_rainfall_projection_h1_kernel(
             )
 
         def scale_z(i):
-            z_bf[i] = rot(work, "z_bf", 2, [P, F], BF16)
+            z_bf[i] = buffer("z_bf", 2, [P, F], BF16)
             nc.vector.tensor_tensor(out=z_bf[i][:], in0=z_diff[i][:], in1=inv_row[:], op=ALU.mult)
 
         def transpose_z(i):
-            bank = rot(psum, "ring", RING, [P, 2, P], F32)
-            z_bank[i] = bank
+            z_bank[i] = bank("ring", RING, [P, 2, P], F32)
             for u in range(2):
-                nc.tensor.transpose(bank[:, u, :], z_bf[i][:].bitcast(F32)[:, P * u : P * (u + 1)], ident[:])
+                nc.tensor.transpose(z_bank[i][:, u, :], z_bf[i][:].bitcast(F32)[:, P * u : P * (u + 1)], ident[:])
 
         def copy_z(i):
-            z_t[i] = rot(work, "z_t", 2, [P, P, 2], F32)
-            nc.scalar.copy(out=z_t[i][:], in_=z_bank[i][:].rearrange("p u m -> p m u"))
+            z_turned[i] = buffer("z_turned", 2, [P, P, 2], F32)
+            nc.scalar.copy(out=z_turned[i][:], in_=z_bank[i][:].rearrange("p u m -> p m u"))
 
         def quantise_z(i):
             c, s = divmod(i, 2)
             if s == 0:
-                z_q[c] = (rot(work, "z_codes", 2, [P, CH], U32), rot(work, "z_scales", 2, [P, CH], U8))
-            codes, scales = z_q[c]
+                z_quant[c] = (buffer("z_codes", 2, [P, CHUNK], U32), buffer("z_scales", 2, [P, CHUNK], U8))
+            codes, scales = z_quant[c]
             nc.vector.quantize_mx(
                 out=codes[:, P * s : P * (s + 1)].bitcast(FP8X4),
                 scales=scales[:, P * s : P * (s + 1)],
-                in_=z_t[i][:].rearrange("p m u -> p (m u)").bitcast(BF16),
+                in_=z_turned[i][:].rearrange("p m u -> p (m u)").bitcast(BF16),
             )
+
+        sums, y_cells, y_bf, y_banks, y_out, y_two = {}, {}, {}, {}, {}, {}
 
         def stage2(un):
-            c, g, m0, w = UNITS[un]
-            codes, scales = z_q[c]
-            per_bank = 512 // w
-            outs = []
-            for t in range(4):
-                if t % per_bank == 0:
-                    bank = rot(psum, "ring", RING, [P, per_bank, w], F32)
-                outs.append(bank[:, t % per_bank, :])
-                nc.tensor.matmul_mx(
-                    out=outs[t],
-                    lhsT=r_words[g][:, t, :].bitcast(FP4X4),
-                    lhsT_scale=r_scales[:, 4 * g + t, :],
-                    rhs=codes[:, m0 : m0 + w].bitcast(FP8X4),
-                    rhs_scale=scales[:, m0 : m0 + w],
-                    start=True,
-                    stop=True,
-                )
-            y_t[un] = rot(work, "y_t", 4, [P, 4, w], F32)
-            sums[un] = outs
+            c, g = divmod(un, RAIN_GROUPS)
+            codes, scales = z_quant[c]
+            sums[un] = []
+            for b in range(2):
+                two_sums = bank("ring", RING, [P, 2, CHUNK], F32)
+                sums[un].append(two_sums)
+                for tt in range(2):
+                    t = 2 * b + tt
+                    nc.tensor.matmul_mx(
+                        out=two_sums[:, tt, :],
+                        lhsT=r_words[g][:, t, :].bitcast(FP4X4),
+                        lhsT_scale=r_scales[:, PACK * g + t, :],
+                        rhs=codes[:].bitcast(FP8X4),
+                        rhs_scale=scales[:],
+                        start=True,
+                        stop=True,
+                    )
+            y_cells[un] = buffer("y_cells", 4, [P, PACK, CHUNK], F32)
 
-        def affine(un, t, on_vector):
-            g = UNITS[un][1]
-            col = slice(4 * g + t, 4 * g + t + 1)
-            if on_vector:
-                nc.vector.tensor_scalar(
-                    out=y_t[un][:, t, :], in0=sums[un][t], scalar1=spread_col[:, col],
-                    scalar2=shift_col[:, col], op0=ALU.mult, op1=ALU.add,
-                )
-            else:
-                nc.scalar.activation(
-                    out=y_t[un][:, t, :], in_=sums[un][t], func=ACT.Identity,
-                    bias=shift_col[:, col], scale=spread_col[:, col],
-                )
+        def affine(un, b, on_vector):
+            g = un % RAIN_GROUPS
+            for tt in range(2):
+                t = 2 * b + tt
+                col = slice(PACK * g + t, PACK * g + t + 1)
+                if on_vector:
+                    nc.vector.tensor_scalar(
+                        out=y_cells[un][:, t, :], in0=sums[un][b][:, tt, :], scalar1=spread_col[:, col],
+                        scalar2=shift_col[:, col], op0=ALU.mult, op1=ALU.add,
+                    )
+                else:
+                    nc.scalar.activation(
+                        out=y_cells[un][:, t, :], in_=sums[un][b][:, tt, :], func=ACT.Identity,
+                        bias=shift_col[:, col], scale=spread_col[:, col],
+                    )
 
         def interleave_y(un):
-            y_bf[un] = rot(work, "y_bf", 3, [P, UNITS[un][3], 4], BF16)
-            nc.vector.tensor_copy(out=y_bf[un][:], in_=y_t[un][:].rearrange("p t m -> p m t"))
+            y_bf[un] = buffer("y_bf", 3, [P, CHUNK, PACK], BF16)
+            nc.vector.tensor_copy(out=y_bf[un][:], in_=y_cells[un][:].rearrange("p t m -> p m t"))
 
         def quantise_y(un):
-            c, g, m0, w = UNITS[un]
-            codes = rot(work, "y_codes", 4, [P, w], U32)
+            c, g = divmod(un, RAIN_GROUPS)
+            codes = buffer("y_codes", 4, [P, CHUNK], U32)
             nc.vector.quantize_mx(
                 out=codes[:].bitcast(FP8X4),
-                scales=y_scales[c // 3][:, g, CH * (c % 3) + m0 : CH * (c % 3) + m0 + w],
+                scales=y_scales[c][:, g, :],
                 in_=y_bf[un][:].rearrange("p m t -> p (m t)"),
             )
-            first = CH * c + m0
-            nc.sync.dma_start(
-                out=out_1[g].rearrange("p m t -> p (m t)")[:, 4 * first : 4 * (first + w)].bitcast(I32),
-                in_=codes[:].bitcast(I32),
-            )
-            if g == 3 and c >= 2:
-                cols = slice(0, 3 * CH) if c == 2 else slice(3 * CH, 4 * CH)
+            words = out_1[g].rearrange("p m t -> p (m t)")[:, PACK * CHUNK * c : PACK * CHUNK * (c + 1)]
+            nc.sync.dma_start(out=words.bitcast(I32), in_=codes[:].bitcast(I32))
+            if g == RAIN_GROUPS - 1:
                 for q in range(4):
+                    rows = out_2[:, 4 * q : 4 * q + 4, CHUNK * c : CHUNK * (c + 1)]
                     nc.sync.dma_start(
-                        out=out_2[:, 4 * q : 4 * q + 4, cols].rearrange("g r m -> r g m").bitcast(I32),
-                        in_=y_scales[c // 3][32 * q : 32 * q + 4].bitcast(I32),
+                        out=rows.rearrange("g r m -> r g m").bitcast(I32),
+                        in_=y_scales[c][32 * q : 32 * q + 4].bitcast(I32),
                     )
 
         def transpose_y(un):
-            w = UNITS[un][3]
-            if un >= 8:
-                y_out[un] = rot(work, "y_out", 4, [P, w // P, 512], F32)
+            if un >= PAIRED_UNITS:
+                y_out[un] = buffer("y_out", 4, [P, 2, GROUP], F32)
             else:
                 if un % 2 == 0:
-                    y_pair[un // 2] = rot(work, "y_pair", 2, [P, w // P, 1024], F32)
-                y_out[un] = y_pair[un // 2][:, :, 512 * (un % 2) : 512 * (un % 2 + 1)]
-            turned[un] = []
-            for s in range(w // P):
-                bank = rot(psum, "ring", RING, [P, 4, P], F32)
-                turned[un].append(bank)
-                for t in range(4):
-                    nc.tensor.transpose(bank[:, t, :], y_t[un][:, t, P * s : P * (s + 1)], ident[:])
+                    y_two[un] = buffer("y_two", 2, [P, 2, 2 * GROUP], F32)
+                y_out[un] = y_two[un - un % 2][:, :, GROUP * (un % 2) : GROUP * (un % 2 + 1)]
+            y_banks[un] = []
+            for s in range(2):
+                turned = bank("ring", RING, [P, PACK, P], F32)
+                y_banks[un].append(turned)
+                for t in range(PACK):
+                    nc.tensor.transpose(turned[:, t, :], y_cells[un][:, t, P * s : P * (s + 1)], ident[:])
 
         def copy_y(un, s, on_vector):
             move(
                 on_vector,
-                y_out[un][:, s, :].rearrange("m (p t) -> m p t", t=4),
-                turned[un][s][:].rearrange("m t p -> m p t"),
+                y_out[un][:, s, :].rearrange("m (p t) -> m p t", t=PACK),
+                y_banks[un][s][:].rearrange("m t p -> m p t"),
             )
 
         def store_y(un, s0, count):
-            c, g, m0, w = UNITS[un]
-            first = CH * c + m0 + P * s0
-            nc.sync.dma_start(
-                out=out_0[first : first + P * count, 512 * g : 512 * (g + 1)].rearrange("(s m) n -> m s n", m=P),
-                in_=y_out[un][:, s0 : s0 + count, :],
-            )
+            c, g = divmod(un, RAIN_GROUPS)
+            first = CHUNK * c + P * s0
+            rows = out_0[first : first + P * count, GROUP * g : GROUP * (g + 1)]
+            nc.sync.dma_start(out=rows.rearrange("(s m) n -> m s n", m=P), in_=y_out[un][:, s0 : s0 + count, :])
 
-        def store_y_pair(un):
-            c, g, m0, w = UNITS[un]
-            nc.sync.dma_start(
-                out=out_0[CH * c : CH * (c + 1), 512 * g : 512 * (g + 2)].rearrange("(s m) n -> m s n", m=P),
-                in_=y_pair[un // 2][:],
-            )
-
-        def spread_rows(col, row):
-            bank = rot(psum, "ring", RING, [P, 4, P], F32)
-            for t in range(4):
-                nc.tensor.transpose(bank[:, t, :], col[:, t : t + 1].to_broadcast([P, P]), ident[:])
-            nc.scalar.copy(
-                out=row[:].rearrange("m (u p e) -> m u p e", u=2, e=2),
-                in_=bank[:].rearrange("m (u e) p -> m u p e", e=2),
-            )
-
-        def permute_r(g):
-            nc.vector.tensor_copy(
-                out=r_words[g][:].rearrange("p t (m b) -> p t m b", b=2),
-                in_=r_raw[:, 1024 * g : 1024 * (g + 1)].rearrange("p (m t b) -> p t m b", t=4, b=2),
-            )
-
-        def permute_r_scales():
-            nc.vector.tensor_copy(
-                out=r_scales[:].rearrange("p (g t) m -> p g t m", t=4),
-                in_=rs_raw[:].rearrange("p (g m t) -> p g t m", g=4, t=4),
-            )
+        def store_y_two(un):
+            c, g = divmod(un, RAIN_GROUPS)
+            rows = out_0[CHUNK * c : CHUNK * (c + 1), GROUP * g : GROUP * (g + 2)]
+            nc.sync.dma_start(out=rows.rearrange("(s m) n -> m s n", m=P), in_=y_two[un][:])
 
         transpose_x(0)
-        copy_x(0, 0, True)
-        copy_x(0, 1, True)
-        spread_rows(centre_col, centre_row)
-        spread_rows(inv_col, inv_row)
+        copy_x(0, 0, ON_SCALAR)
+        copy_x(0, 1, ON_VECTOR)
         quantise_x(0)
         transpose_x(1)
-        copy_x(1, 0, False)
-        copy_x(1, 1, False)
+        copy_x(1, 0, ON_SCALAR)
+        copy_x(1, 1, ON_SCALAR)
+        turn_vectors()
         stage1(0)
+        repeat_on_partitions(CENTRE_ROW, centre_row)
+        repeat_on_partitions(INV_ROW, inv_row)
         quantise_x(1)
+        reorder_r_scales()
         transpose_x(2)
-        copy_x(2, 0, False)
-        copy_x(2, 1, False)
-        split_words(3)
+        copy_x(2, 0, ON_SCALAR)
+        copy_x(2, 1, ON_SCALAR)
         stage1(1)
-        permute_r_scales()
         quantise_x(2)
         centre_z(0)
+        reorder_r_words(0)
         transpose_x(3)
-        split_words(4)
-        copy_x(3, 0, False)
-        copy_x(3, 1, False)
+        copy_x(3, 0, ON_SCALAR)
+        copy_x(3, 1, ON_SCALAR)
         stage1(2)
         scale_z(0)
         quantise_x(3)
-        split_words(5)
-        permute_r(0)
-        permute_r(1)
-        for i in range(2, 8):
-            a0, a1 = 2 * (i - 3), 2 * (i - 3) + 1
-            b0, b1 = a0 - 2, a1 - 2
-            ha, hb = 2 * i, 2 * i + 1
-            zi = i - 2
-            if i > 2:
-                centre_z(zi)
-            transpose_x(ha)
-            copy_x(ha, 0, False)
-            copy_x(ha, 1, False)
-            transpose_x(hb)
-            copy_x(hb, 0, False)
-            if b0 >= 0:
-                interleave_y(b0)
-            if i > 2:
-                scale_z(zi)
-            if i == 4:
-                permute_r(3)
-            copy_x(hb, 1, XV and i > 3)
-            quantise_x(ha)
-            if b0 >= 0:
-                transpose_y(b0)
-                transpose_y(b1)
-            transpose_z(zi)
-            if b0 >= 0:
-                copy_y(b0, 0, False)
-                quantise_y(b0)
-                interleave_y(b1)
-            copy_z(zi)
-            if b0 >= 0:
-                copy_y(b0, 1, True)
-            quantise_z(zi)
-            if b0 >= 0:
-                copy_y(b1, 0, False)
-                copy_y(b1, 1, False)
-                store_y_pair(b0)
-            quantise_x(hb)
-            if b0 >= 0:
-                quantise_y(b1)
-            if i == 2:
-                nc.vector.tensor_copy(out=spread_col[:], in_=spread_raw[:].rearrange("p g t -> p (g t)"))
-                nc.vector.tensor_tensor(
-                    out=shift_col[:], in0=bias_raw[:].rearrange("p g t -> p (g t)"),
-                    in1=spread_raw[:].rearrange("p g t -> p (g t)"), op=ALU.mult,
-                )
-            if i < 7:
-                split_words(ha + 2)
-                split_words(hb + 2)
-            if i == 3:
-                permute_r(2)
-            if i > 2:
-                stage1(ha - 2)
-            if a0 >= 0:
-                stage2(a0)
-                stage2(a1)
-            stage1(hb - 2)
-            if a0 >= 0:
-                for t in range(4):
-                    affine(a0, t, False)
-                for t in range(4):
-                    affine(a1, t, t >= AV)
+        reorder_r_words(1)
+        gather_pairs(5)
 
-        centre_z(6)
-        transpose_y(8)
-        interleave_y(8)
-        copy_y(8, 0, False)
-        scale_z(6)
-        transpose_y(9)
-        copy_y(8, 1, False)
-        store_y(8, 0, 2)
+        FIRST_STEP = 2
+        FIRST_STAGE2_STEP = 3
+        for i in range(FIRST_STEP, TILES):
+            first, second = 2 * i, 2 * i + 1
+            new = 2 * (i - FIRST_STAGE2_STEP)
+            old = new - 2
+            if i > FIRST_STEP:
+                centre_z(i - 2)
+            transpose_x(first)
+            copy_x(first, 0, ON_SCALAR)
+            copy_x(first, 1, ON_SCALAR)
+            transpose_x(second)
+            copy_x(second, 0, ON_SCALAR)
+            if old >= 0:
+                interleave_y(old)
+            if i > FIRST_STEP:
+                scale_z(i - 2)
+            copy_x(second, 1, ON_SCALAR)
+            quantise_x(first)
+            if old >= 0:
+                transpose_y(old)
+                transpose_y(old + 1)
+            transpose_z(i - 2)
+            if old >= 0:
+                copy_y(old, 0, ON_SCALAR)
+                quantise_y(old)
+                interleave_y(old + 1)
+            copy_z(i - 2)
+            if old >= 0:
+                copy_y(old, 1, ON_VECTOR)
+            quantise_z(i - 2)
+            if old >= 0:
+                copy_y(old + 1, 0, ON_SCALAR)
+                copy_y(old + 1, 1, ON_SCALAR)
+                store_y_two(old)
+            quantise_x(second)
+            if old >= 0:
+                quantise_y(old + 1)
+            gather_pairs(first + 2)
+            gather_pairs(second + 2)
+            if i == FIRST_STAGE2_STEP:
+                reorder_r_words(2)
+                reorder_r_words(3)
+            if i > FIRST_STEP:
+                stage1(first - 2)
+            if new >= 0:
+                stage2(new)
+                stage2(new + 1)
+            stage1(second - 2)
+            if new >= 0:
+                for un in (new, new + 1):
+                    affine(un, 0, ON_SCALAR)
+                    affine(un, 1, ON_SCALAR)
+
+        last = TILES - 1
         stage2(10)
-        stage1(14)
-        stage1(15)
+        transpose_y(8)
+        transpose_y(9)
+        centre_z(last - 1)
+        interleave_y(8)
+        affine(10, 0, ON_SCALAR)
+        stage1(2 * last)
+        stage1(2 * last + 1)
+        copy_y(8, 0, ON_SCALAR)
+        copy_y(8, 1, ON_VECTOR)
+        store_y(8, 0, 2)
+        copy_y(9, 0, ON_SCALAR)
+        affine(10, 1, ON_SCALAR)
+        scale_z(last - 1)
+        transpose_z(last - 1)
         quantise_y(8)
         interleave_y(9)
-        copy_y(9, 0, False)
-        copy_y(9, 1, False)
+        copy_y(9, 1, ON_SCALAR)
         store_y(9, 0, 2)
-        affine(10, 2, True)
-        affine(10, 3, True)
-        affine(10, 0, False)
-        affine(10, 1, False)
-        quantise_y(9)
         stage2(11)
-        centre_z(7)
-        transpose_z(6)
+        copy_z(last - 1)
+        affine(11, 0, ON_SCALAR)
+        centre_z(last)
+        quantise_y(9)
+        scale_z(last)
         transpose_y(10)
-        affine(11, 0, False)
-        affine(11, 1, False)
+        affine(11, 1, ON_SCALAR)
+        transpose_z(last)
+        transpose_y(11)
+        copy_z(last)
+        quantise_z(last - 1)
         interleave_y(10)
-        scale_z(7)
-        transpose_z(7)
-        copy_z(6)
-        affine(11, 2, False)
-        copy_z(7)
-        quantise_z(6)
-        affine(11, 3, True)
-        quantise_z(7)
-        copy_y(10, 0, False)
-        quantise_y(10)
-        copy_y(10, 1, True)
+        copy_y(10, 0, ON_SCALAR)
+        quantise_z(last)
+        copy_y(10, 1, ON_SCALAR)
         store_y(10, 0, 2)
-        last = len(UNITS) - 1
-        for un in range(11, last + 1):
-            if un < last:
-                stage2(un + 1)
-            transpose_y(un)
-            interleave_y(un)
-            if un < last:
-                for t in range(4):
-                    affine(un + 1, t, t >= 2)
-            copy_y(un, 0, False)
-            if un < last:
-                quantise_y(un)
-                copy_y(un, 1, False)
-                store_y(un, 0, 2)
+
+        LAST_OF_CHUNK_2 = 11
+        for un in range(LAST_OF_CHUNK_2, UNITS - 1):
+            stage2(un + 1)
+            if un == LAST_OF_CHUNK_2:
+                quantise_y(un - 1)
             else:
-                store_y(un, 0, 1)
-                copy_y(un, 1, True)
-                store_y(un, 1, 1)
-                quantise_y(un)
+                transpose_y(un)
+            interleave_y(un)
+            affine(un + 1, 0, ON_SCALAR)
+            affine(un + 1, 1, ON_VECTOR)
+            copy_y(un, 0, ON_SCALAR)
+            quantise_y(un)
+            copy_y(un, 1, ON_SCALAR)
+            store_y(un, 0, 2)
+
+        un = UNITS - 1
+        transpose_y(un)
+        interleave_y(un)
+        copy_y(un, 0, ON_SCALAR)
+        quantise_y(un)
+        store_y(un, 0, 1)
+        copy_y(un, 1, ON_VECTOR)
+        store_y(un, 1, 1)

from contextlib import ExitStack

import concourse.mybir as mybir
from concourse.masks import make_identity

M, C, F, N = 1024, 4096, 512, 2048
FLOPS = 2 * M * C * F + 2 * M * F * N

F32 = mybir.dt.float32
BF16 = mybir.dt.bfloat16
I32 = mybir.dt.int32
U32 = mybir.dt.uint32
U8 = mybir.dt.uint8
FP8X4 = mybir.dt.float8_e4m3fn_x4
FP4X4 = mybir.dt.float4_e2m1fn_x4
ALU = mybir.AluOpType
ACT = mybir.ActivationFunctionType

P = 128
PACK = 4
GROUP = P * PACK
HALF = C // 2
CHUNK = 2 * P
TILES = M // P
HALVES = 2 * TILES
RAIN_GROUPS = N // GROUP
UNITS = (M // CHUNK) * RAIN_GROUPS
RING = 7
FINE_TILES = 4
PAIRED_UNITS = 8

GATHER_ON_SCALAR = (5, 7, 9)
GATHER_ON_VECTOR = range(10, HALVES)

SPREAD_ROW, BIAS_ROW, CENTRE_ROW, INV_ROW, VECTOR_ROWS = 0, 4, 8, 9, 10

ON_VECTOR, ON_SCALAR = True, False


def tile_sst_pattern_rainfall_projection_h1_kernel(
    tc, sst, patterns_words, patterns_scales, centre, inv_scale,
    regression_words, regression_scales, bias, rain_spread, out_0, out_1, out_2,
):
    nc = tc.nc
    with ExitStack() as ctx:
        keep = ctx.enter_context(tc.tile_pool(name="keep", bufs=1))
        work = ctx.enter_context(tc.tile_pool(name="work", bufs=1))
        psum = ctx.enter_context(tc.psum_pool(name="psum", bufs=1))
        ctx.enter_context(tc.manual_schedule())

        uses = {}

        def next_slot(kind, depth):
            count = uses.get(kind, 0)
            uses[kind] = count + 1
            return "%s%d" % (kind, count % depth)

        def buffer(kind, depth, shape, dtype):
            slot = next_slot(kind, depth)
            return work.tile(shape, dtype, name=slot, tag=slot, align_bytes=64)

        def bank(kind, depth, shape, dtype):
            slot = next_slot(kind, depth)
            return psum.tile(shape, dtype, name=slot, tag=slot)

        ident = keep.tile([P, P], F32, align_bytes=64)
        ident_bf = keep.tile([P, P], BF16, align_bytes=64)
        e_words = [keep.tile([P, 4, 2 * F], U8, name="e_words%d" % j, align_bytes=64) for j in range(2)]
        e_scales = [keep.tile([P, 4, F], U8, name="e_scales%d" % j, align_bytes=64) for j in range(2)]
        r_loaded = [keep.tile([P, N], U8, name="r_loaded%d" % j, align_bytes=64) for j in range(2)]
        r_scales_loaded = keep.tile([P, N], U8, align_bytes=64)
        r_words = [keep.tile([P, PACK, 2 * P], U8, name="r_words%d" % g, align_bytes=64) for g in range(RAIN_GROUPS)]
        r_scales = keep.tile([P, RAIN_GROUPS * PACK, P], U8, name="r_scales", align_bytes=64)
        vector_rows = keep.tile([P, GROUP], BF16, align_bytes=64)
        vector_cols = keep.tile([P, VECTOR_ROWS, PACK], F32, align_bytes=64)
        spread_col = vector_cols[:, SPREAD_ROW:BIAS_ROW, :].rearrange("p g t -> p (g t)")
        shift_col = keep.tile([P, RAIN_GROUPS * PACK], F32, align_bytes=64)
        centre_row = keep.tile([P, F], F32, align_bytes=64)
        inv_row = keep.tile([P, F], F32, align_bytes=64)
        y_scales = [
            keep.tile([P, RAIN_GROUPS, CHUNK], U8, name="y_scales%d" % c, align_bytes=64) for c in range(M // CHUNK)
        ]

        nc.vector.memset(vector_rows[:], 0.0)
        nc.vector.memset(e_scales[0][:].rearrange("p g n -> p (g n)").bitcast(I32), 0)
        nc.vector.memset(e_scales[1][:].rearrange("p g n -> p (g n)").bitcast(I32), 0)
        nc.vector.memset(r_scales_loaded[:].bitcast(I32), 0)
        make_identity(nc, ident[:])
        nc.scalar.activation(out=ident_bf[:], in_=ident[:], func=ACT.Identity)

        x_raw = {}

        def load_half(h):
            i, j = divmod(h, 2)
            x_raw[h] = buffer("x_raw", 2 * FINE_TILES, [P, HALF], BF16)
            nc.sync.dma_start(out=x_raw[h][:], in_=sst[P * i : P * (i + 1), HALF * j : HALF * (j + 1)])

        def load_tile(i):
            both = buffer("x_tile", TILES - FINE_TILES, [P, C], BF16)
            nc.sync.dma_start(out=both[:], in_=sst[P * i : P * (i + 1), :])
            x_raw[2 * i] = both[:, :HALF]
            x_raw[2 * i + 1] = both[:, HALF:]

        def load_e_words(j):
            nc.sync.dma_start(
                out=e_words[j][:].bitcast(I32),
                in_=patterns_words[4 * j : 4 * j + 4].rearrange("g p n -> p g n").bitcast(I32),
            )

        def load_e_scales(j):
            for q in range(4):
                rows = patterns_scales[4 * j : 4 * j + 4, 4 * q : 4 * q + 4, :]
                nc.sync.dma_start(
                    out=e_scales[j][32 * q : 32 * q + 4].bitcast(I32),
                    in_=rows.rearrange("g r n -> r g n").bitcast(I32),
                )

        def load_r_scales():
            for q in range(4):
                nc.sync.dma_start(
                    out=r_scales_loaded[32 * q : 32 * q + 4, :].bitcast(I32),
                    in_=regression_scales[0, 4 * q : 4 * q + 4, :].bitcast(I32),
                )

        def load_r_words(j):
            nc.sync.dma_start(
                out=r_loaded[j][:].bitcast(I32), in_=regression_words[0, :, N * j : N * (j + 1)].bitcast(I32)
            )

        def load_vectors():
            for row, vec, rows in (
                (SPREAD_ROW, rain_spread, RAIN_GROUPS),
                (BIAS_ROW, bias, RAIN_GROUPS),
                (CENTRE_ROW, centre, 1),
                (INV_ROW, inv_scale, 1),
            ):
                nc.sync.dma_start(out=vector_rows[row : row + rows, :], in_=vec.rearrange("(g n) -> g n", g=rows))

        load_half(0)
        load_vectors()
        load_half(1)
        load_e_scales(0)
        load_e_words(0)
        load_r_scales()
        load_half(2)
        load_e_scales(1)
        load_e_words(1)
        load_half(3)
        load_r_words(0)
        load_half(4)
        load_half(5)
        load_r_words(1)
        load_half(6)
        load_half(7)
        for i in range(FINE_TILES, TILES):
            load_tile(i)

        def move(on_vector, dst, src):
            if on_vector:
                nc.vector.tensor_copy(out=dst, in_=src)
            else:
                nc.scalar.copy(out=dst, in_=src)

        def turn_vectors():
            turned_rows = bank("ring", RING, [P, PACK, P], BF16)
            for t in range(PACK):
                nc.tensor.transpose(turned_rows[:, t, :], vector_rows[:, t:GROUP:PACK], ident_bf[:])
            nc.vector.tensor_copy(
                out=vector_cols[:], in_=turned_rows[:, :, 0:VECTOR_ROWS].rearrange("p t r -> p r t")
            )
            nc.vector.tensor_tensor(
                out=shift_col[:],
                in0=vector_cols[:, BIAS_ROW:CENTRE_ROW, :].rearrange("p g t -> p (g t)"),
                in1=spread_col,
                op=ALU.mult,
            )

        def repeat_on_partitions(r, row):
            repeated = bank("ring", RING, [P, PACK, P], F32)
            for t in range(PACK):
                nc.tensor.transpose(repeated[:, t, :], vector_cols[:, r, t : t + 1].to_broadcast([P, P]), ident[:])
            nc.scalar.copy(
                out=row[:].rearrange("m (u p e) -> m u p e", u=2, e=2),
                in_=repeated[:].rearrange("m (u e) p -> m u p e", e=2),
            )

        def reorder_r_words(g):
            loaded = r_loaded[g // 2][:, 2 * GROUP * (g % 2) : 2 * GROUP * (g % 2 + 1)]
            nc.vector.tensor_copy(
                out=r_words[g][:].rearrange("k t (p b) -> k t p b", b=2),
                in_=loaded.rearrange("k (p t b) -> k t p b", t=PACK, b=2),
            )

        def reorder_r_scales():
            nc.vector.tensor_copy(
                out=r_scales[:].rearrange("k (g t) p -> k g t p", t=PACK),
                in_=r_scales_loaded[:].rearrange("k (g p t) -> k g t p", g=RAIN_GROUPS, t=PACK),
            )

        x_gathered, x_banks, x_turned, x_quant = {}, {}, {}, {}
        acc, z_diff, z_bf, z_bank, z_turned, z_quant = {}, {}, {}, {}, {}, {}

        def gather_pairs(h):
            if h in GATHER_ON_VECTOR or h in GATHER_ON_SCALAR:
                x_gathered[h] = buffer("x_gathered", 4, [P, 2, HALF // 4], F32)
                move(
                    h in GATHER_ON_VECTOR,
                    x_gathered[h][:].rearrange("m u (c i) -> m c u i", i=4),
                    x_raw[h][:].bitcast(F32).rearrange("m (c i u) -> m c u i", i=4, u=2),
                )

        def transpose_x(h):
            x_turned[h] = buffer("x_turned", 4, [P, 4, P, 2], F32)
            x_banks[h] = []
            for b in range(2):
                turned = bank("ring", RING, [P, 2, 2, P], F32)
                x_banks[h].append(turned)
                for gg in range(2):
                    g = 2 * b + gg
                    for u in range(2):
                        if h in x_gathered:
                            pairs = x_gathered[h][:, u, P * g : P * (g + 1)]
                        else:
                            pairs = x_raw[h][:].bitcast(F32)[:, 2 * P * g + u : 2 * P * (g + 1) : 2]
                        nc.tensor.transpose(turned[:, gg, u, :], pairs, ident[:])

        def copy_x(h, b, on_vector):
            move(on_vector, x_turned[h][:, 2 * b : 2 * b + 2], x_banks[h][b][:].rearrange("p g u m -> p g m u"))

        def quantise_x(h):
            codes = buffer("x_codes", 4, [P, 4 * P], U32)
            scales = buffer("x_scales", 4, [P, 4 * P], U8)
            x_quant[h] = (codes, scales)
            nc.vector.quantize_mx(
                out=codes[:].bitcast(FP8X4),
                scales=scales[:],
                in_=x_turned[h][:].rearrange("p g m u -> p (g m u)").bitcast(BF16),
            )

        def stage1(h):
            i, j = divmod(h, 2)
            if j == 0:
                acc[i] = bank("acc", 1, [P, F], F32)
            codes, scales = x_quant[h]
            for gg in range(4):
                nc.tensor.matmul_mx(
                    out=acc[i][:],
                    lhsT=codes[:, P * gg : P * (gg + 1)].bitcast(FP8X4),
                    lhsT_scale=scales[:, P * gg : P * (gg + 1)],
                    rhs=e_words[j][:, gg, :].bitcast(FP4X4),
                    rhs_scale=e_scales[j][:, gg, :],
                    start=(j == 0 and gg == 0),
                    stop=(j == 1 and gg == 3),
                )

        def centre_z(i):
            z_diff[i] = buffer("z_diff", 1, [P, F], F32)
            nc.vector.tensor_tensor(
                out=z_diff[i][:].rearrange("m (u p e) -> m u p e", u=2, e=2),
                in0=acc[i][:].rearrange("m (p u e) -> m u p e", u=2, e=2),
                in1=centre_row[:].rearrange("m (u p e) -> m u p e", u=2, e=2),
                op=ALU.subtract,
            )

        def scale_z(i):
            z_bf[i] = buffer("z_bf", 2, [P, F], BF16)
            nc.vector.tensor_tensor(out=z_bf[i][:], in0=z_diff[i][:], in1=inv_row[:], op=ALU.mult)

        def transpose_z(i):
            z_bank[i] = bank("ring", RING, [P, 2, P], F32)
            for u in range(2):
                nc.tensor.transpose(z_bank[i][:, u, :], z_bf[i][:].bitcast(F32)[:, P * u : P * (u + 1)], ident[:])

        def copy_z(i):
            z_turned[i] = buffer("z_turned", 2, [P, P, 2], F32)
            nc.scalar.copy(out=z_turned[i][:], in_=z_bank[i][:].rearrange("p u m -> p m u"))

        def quantise_z(i):
            c, s = divmod(i, 2)
            if s == 0:
                z_quant[c] = (buffer("z_codes", 2, [P, CHUNK], U32), buffer("z_scales", 2, [P, CHUNK], U8))
            codes, scales = z_quant[c]
            nc.vector.quantize_mx(
                out=codes[:, P * s : P * (s + 1)].bitcast(FP8X4),
                scales=scales[:, P * s : P * (s + 1)],
                in_=z_turned[i][:].rearrange("p m u -> p (m u)").bitcast(BF16),
            )

        sums, y_cells, y_bf, y_banks, y_out, y_two = {}, {}, {}, {}, {}, {}

        def stage2(un):
            c, g = divmod(un, RAIN_GROUPS)
            codes, scales = z_quant[c]
            sums[un] = []
            for b in range(2):
                two_sums = bank("ring", RING, [P, 2, CHUNK], F32)
                sums[un].append(two_sums)
                for tt in range(2):
                    t = 2 * b + tt
                    nc.tensor.matmul_mx(
                        out=two_sums[:, tt, :],
                        lhsT=r_words[g][:, t, :].bitcast(FP4X4),
                        lhsT_scale=r_scales[:, PACK * g + t, :],
                        rhs=codes[:].bitcast(FP8X4),
                        rhs_scale=scales[:],
                        start=True,
                        stop=True,
                    )
            y_cells[un] = buffer("y_cells", 4, [P, PACK, CHUNK], F32)

        def affine(un, b, on_vector):
            g = un % RAIN_GROUPS
            for tt in range(2):
                t = 2 * b + tt
                col = slice(PACK * g + t, PACK * g + t + 1)
                if on_vector:
                    nc.vector.tensor_scalar(
                        out=y_cells[un][:, t, :], in0=sums[un][b][:, tt, :], scalar1=spread_col[:, col],
                        scalar2=shift_col[:, col], op0=ALU.mult, op1=ALU.add,
                    )
                else:
                    nc.scalar.activation(
                        out=y_cells[un][:, t, :], in_=sums[un][b][:, tt, :], func=ACT.Identity,
                        bias=shift_col[:, col], scale=spread_col[:, col],
                    )

        def interleave_y(un):
            y_bf[un] = buffer("y_bf", 3, [P, CHUNK, PACK], BF16)
            nc.vector.tensor_copy(out=y_bf[un][:], in_=y_cells[un][:].rearrange("p t m -> p m t"))

        def quantise_y(un):
            c, g = divmod(un, RAIN_GROUPS)
            codes = buffer("y_codes", 4, [P, CHUNK], U32)
            nc.vector.quantize_mx(
                out=codes[:].bitcast(FP8X4),
                scales=y_scales[c][:, g, :],
                in_=y_bf[un][:].rearrange("p m t -> p (m t)"),
            )
            words = out_1[g].rearrange("p m t -> p (m t)")[:, PACK * CHUNK * c : PACK * CHUNK * (c + 1)]
            nc.sync.dma_start(out=words.bitcast(I32), in_=codes[:].bitcast(I32))
            if g == RAIN_GROUPS - 1:
                for q in range(4):
                    rows = out_2[:, 4 * q : 4 * q + 4, CHUNK * c : CHUNK * (c + 1)]
                    nc.sync.dma_start(
                        out=rows.rearrange("g r m -> r g m").bitcast(I32),
                        in_=y_scales[c][32 * q : 32 * q + 4].bitcast(I32),
                    )

        def transpose_y(un):
            if un >= PAIRED_UNITS:
                y_out[un] = buffer("y_out", 4, [P, 2, GROUP], F32)
            else:
                if un % 2 == 0:
                    y_two[un] = buffer("y_two", 2, [P, 2, 2 * GROUP], F32)
                y_out[un] = y_two[un - un % 2][:, :, GROUP * (un % 2) : GROUP * (un % 2 + 1)]
            y_banks[un] = []
            for s in range(2):
                turned = bank("ring", RING, [P, PACK, P], F32)
                y_banks[un].append(turned)
                for t in range(PACK):
                    nc.tensor.transpose(turned[:, t, :], y_cells[un][:, t, P * s : P * (s + 1)], ident[:])

        def copy_y(un, s, on_vector):
            move(
                on_vector,
                y_out[un][:, s, :].rearrange("m (p t) -> m p t", t=PACK),
                y_banks[un][s][:].rearrange("m t p -> m p t"),
            )

        def store_y(un, s0, count):
            c, g = divmod(un, RAIN_GROUPS)
            first = CHUNK * c + P * s0
            rows = out_0[first : first + P * count, GROUP * g : GROUP * (g + 1)]
            nc.sync.dma_start(out=rows.rearrange("(s m) n -> m s n", m=P), in_=y_out[un][:, s0 : s0 + count, :])

        def store_y_two(un):
            c, g = divmod(un, RAIN_GROUPS)
            rows = out_0[CHUNK * c : CHUNK * (c + 1), GROUP * g : GROUP * (g + 2)]
            nc.sync.dma_start(out=rows.rearrange("(s m) n -> m s n", m=P), in_=y_two[un][:])

        transpose_x(0)
        copy_x(0, 0, ON_SCALAR)
        copy_x(0, 1, ON_VECTOR)
        quantise_x(0)
        transpose_x(1)
        copy_x(1, 0, ON_SCALAR)
        copy_x(1, 1, ON_SCALAR)
        turn_vectors()
        stage1(0)
        repeat_on_partitions(CENTRE_ROW, centre_row)
        repeat_on_partitions(INV_ROW, inv_row)
        quantise_x(1)
        reorder_r_scales()
        transpose_x(2)
        copy_x(2, 0, ON_SCALAR)
        copy_x(2, 1, ON_SCALAR)
        stage1(1)
        quantise_x(2)
        centre_z(0)
        reorder_r_words(0)
        transpose_x(3)
        copy_x(3, 0, ON_SCALAR)
        copy_x(3, 1, ON_SCALAR)
        stage1(2)
        scale_z(0)
        quantise_x(3)
        reorder_r_words(1)
        gather_pairs(5)

        FIRST_STEP = 2
        FIRST_STAGE2_STEP = 3
        for i in range(FIRST_STEP, TILES):
            first, second = 2 * i, 2 * i + 1
            new = 2 * (i - FIRST_STAGE2_STEP)
            old = new - 2
            if i > FIRST_STEP:
                centre_z(i - 2)
            transpose_x(first)
            copy_x(first, 0, ON_SCALAR)
            copy_x(first, 1, ON_SCALAR)
            transpose_x(second)
            copy_x(second, 0, ON_SCALAR)
            if old >= 0:
                interleave_y(old)
            if i > FIRST_STEP:
                scale_z(i - 2)
            copy_x(second, 1, ON_SCALAR)
            quantise_x(first)
            if old >= 0:
                transpose_y(old)
                transpose_y(old + 1)
            transpose_z(i - 2)
            if old >= 0:
                copy_y(old, 0, ON_SCALAR)
                quantise_y(old)
                interleave_y(old + 1)
            copy_z(i - 2)
            if old >= 0:
                copy_y(old, 1, ON_VECTOR)
            quantise_z(i - 2)
            if old >= 0:
                copy_y(old + 1, 0, ON_SCALAR)
                copy_y(old + 1, 1, ON_SCALAR)
                store_y_two(old)
            quantise_x(second)
            if old >= 0:
                quantise_y(old + 1)
            gather_pairs(first + 2)
            gather_pairs(second + 2)
            if i == FIRST_STAGE2_STEP:
                reorder_r_words(2)
                reorder_r_words(3)
            if i > FIRST_STEP:
                stage1(first - 2)
            if new >= 0:
                stage2(new)
                stage2(new + 1)
            stage1(second - 2)
            if new >= 0:
                for un in (new, new + 1):
                    affine(un, 0, ON_SCALAR)
                    affine(un, 1, ON_SCALAR)

        last = TILES - 1
        stage2(10)
        transpose_y(8)
        transpose_y(9)
        centre_z(last - 1)
        interleave_y(8)
        affine(10, 0, ON_SCALAR)
        stage1(2 * last)
        stage1(2 * last + 1)
        copy_y(8, 0, ON_SCALAR)
        copy_y(8, 1, ON_VECTOR)
        store_y(8, 0, 2)
        copy_y(9, 0, ON_SCALAR)
        affine(10, 1, ON_SCALAR)
        scale_z(last - 1)
        transpose_z(last - 1)
        quantise_y(8)
        interleave_y(9)
        copy_y(9, 1, ON_SCALAR)
        store_y(9, 0, 2)
        stage2(11)
        copy_z(last - 1)
        affine(11, 0, ON_SCALAR)
        centre_z(last)
        quantise_y(9)
        scale_z(last)
        transpose_y(10)
        affine(11, 1, ON_SCALAR)
        transpose_z(last)
        transpose_y(11)
        copy_z(last)
        quantise_z(last - 1)
        interleave_y(10)
        copy_y(10, 0, ON_SCALAR)
        quantise_z(last)
        copy_y(10, 1, ON_SCALAR)
        store_y(10, 0, 2)

        LAST_OF_CHUNK_2 = 11
        for un in range(LAST_OF_CHUNK_2, UNITS - 1):
            stage2(un + 1)
            if un == LAST_OF_CHUNK_2:
                quantise_y(un - 1)
            else:
                transpose_y(un)
            interleave_y(un)
            affine(un + 1, 0, ON_SCALAR)
            affine(un + 1, 1, ON_VECTOR)
            copy_y(un, 0, ON_SCALAR)
            quantise_y(un)
            copy_y(un, 1, ON_SCALAR)
            store_y(un, 0, 2)

        un = UNITS - 1
        transpose_y(un)
        interleave_y(un)
        copy_y(un, 0, ON_SCALAR)
        quantise_y(un)
        store_y(un, 0, 1)
        copy_y(un, 1, ON_VECTOR)
        store_y(un, 1, 1)
